import numpy as np, ml_dtypes
CORES = [10,34,74,98]
N = 4
import mx_ref
BF = ml_dtypes.bfloat16
def entries(a):
    return np.ascontiguousarray(a.T).reshape(-1)
def table(e):
    return np.ascontiguousarray(np.reshape(e, (-1, 16)).T).astype(np.int32)
def gcols(t, e):
    v = np.concatenate([t.reshape(8, 16, -1, 4), np.zeros((8, 16, 1, 4), BF)], axis=2)
    return np.ascontiguousarray(np.stack([v[g][:, e[g]] for g in range(8)])).reshape(128, -1)
def tile(rs):
    return np.stack(rs, axis=2).reshape(128, -1).astype(BF)
def pick(q, e):
    c = np.concatenate([q[0].reshape(128, -1, 4), np.zeros((128, 1, 4), np.uint8)], axis=1); s = np.concatenate([q[1], np.ones((16, 1), np.uint8)], axis=1)
    return (np.ascontiguousarray(c[:, e].reshape(128, -1)), np.ascontiguousarray(s[:, e]))
def join(*qs):
    return (np.concatenate([q[0] for q in qs], axis=1), np.concatenate([q[1] for q in qs], axis=1))
def put(q, e, v):
    c, s = q[0].reshape(128, -1, 4).copy(), q[1].copy(); c[:, e] = v[0].reshape(128, -1, 4); s[:, e] = v[1]
    return (c.reshape(128, -1), s)
def pk(c, s):
    return (np.ascontiguousarray(c), mx_ref.live(s))
def emit(q):
    return q[0], q[1]
def packed(v, rng):
    q = [mx_ref.quantize(np.ascontiguousarray(v[r])) for r in range(N)]
    return np.stack([a for a, b in q]), np.stack([mx_ref.plane(b, rng) for a, b in q])
def values_of_codes():
    e, c = np.zeros((128, 128, 4), np.float32), np.zeros((128, 2, 4), np.uint8)
    e[np.arange(128), np.arange(128), 0] = 1
    c[:127, :, 0] = np.arange(256).reshape(2, 128).T[:127]
    return mx_ref.matmul(mx_ref.quantize(e.reshape(128, 512).astype(BF)), (c.reshape(128, 8), np.full((16, 2), 127, np.uint8))).T.reshape(-1).astype(np.float64)
CODE_VALUE, SCALE_VALUE = values_of_codes(), 2.0 ** (np.arange(256) - 127.0)
def decode(q):
    return (CODE_VALUE[q[0]].reshape(16, 8, -1, 4) * SCALE_VALUE[q[1]][:, None, :, None] + 0.0).reshape(128, -1).astype(np.float32)
def f(rng, *shape):
    return mx_ref.flush((rng.standard_normal(shape, dtype=np.float32) * np.exp2(rng.integers(-2, 3, shape[:-1] + (1,)))).astype(BF))
def wide(rng, *shape, cols=0):
    v = rng.standard_normal(shape, dtype=np.float32) * np.exp2(rng.integers(-12, 13, shape)).astype(np.float32)
    if cols: v *= np.repeat(np.exp2(rng.integers(-cols, cols + 1, shape[:-2] + (1, shape[-1] // 4))) * (rng.random(shape[:-2] + (1, shape[-1] // 4)) > 0.0625), 4, axis=-1).astype(np.float32)
    return mx_ref.flush(v.astype(BF))
C, R = 384, 2
M = N * C
def numbers_of(rng):
    return {"x": np.array(f(rng, N, 128, 4 * C)), "u": np.array(f(rng, N, 128, 512)), "v": np.array(f(rng, N, 128, 512))}
def weights(rng, w):
    c, p = packed(w, rng)
    return {"wc": c, "ws": p}
def still(rng):
    w = np.zeros((N, 128, 4, 128, 4), np.float32)
    i = np.arange(128)
    for b in range(4): w[:, i, b, i, b] = 32
    return weights(rng, w.reshape(N, 128, 2048).astype(BF))
def anywhere(rng):
    return rng.integers(0, M, (4, M))
def stored(e):
    return np.stack([table(e[:, C * r:C * r + C].reshape(-1)) for r in range(N)])
def signs(rng):
    return rng.permutation(N) % 2 * 2.0 - 1.0
def setup_inputs(rng):
    return {**numbers_of(rng), **weights(rng, f(rng, N, 128, 2048)), "sc": stored(anywhere(rng))}
def setup_inputs_ties(rng):
    d = numbers_of(rng)
    x = d["x"].reshape(N, 128, C, 4)
    a = x[0, :8, :3].copy()
    a[:, 2] = 0
    for r in range(N): x[r, :8] = a[:, rng.permutation(C) % 3]
    u = d["u"].reshape(N, 128, 128, 4)
    u[:, :8, 0] = u[0, :8, 0].copy()
    u[:, 8:, 0] = 0
    w = np.array(f(rng, 128, 2048)).reshape(128, 4, 128, 4)
    w[8:, :, :8] = 0
    return {"x": x.reshape(N, 128, 4 * C), "u": u.reshape(N, 128, 512), "v": d["v"], **weights(rng, np.stack([w.reshape(128, 2048)] * N)), "sc": stored(anywhere(rng))}
def setup_inputs_near(rng):
    d = numbers_of(rng)
    g = signs(rng)
    low = np.repeat(g < 0, C)
    o = np.concatenate([rng.permutation(np.flatnonzero(low)), rng.permutation(np.flatnonzero(~low))])
    place = np.argsort(o)
    s = place % (M // 2)
    x = np.abs(d["x"].astype(np.float32)).reshape(N, 128, C, 4)
    v = (((s[:, None] >> np.arange(12)) & 1) * np.exp2(np.arange(12) - 23.0)).reshape(N, C, 12)
    x[:, :8] = 0
    x[:, 0, :, 0] = 1
    for i in range(3): x[:, 8 + i] = v[:, :, 4 * i:4 * i + 4]
    x[:, 11:16] = rng.integers(4, 8, (N, 5, C, 4)) * 2.0 ** -20
    u = d["u"].reshape(N, 128, 128, 4)
    u[:, :, 0] = 0
    u[:, 0, 0, 0] = g.astype(np.float32).astype(BF)
    u[:, 8:11, 0] = 1
    c = rng.permutation(M)
    after = np.zeros(M, int)
    after[c] = np.roll(c, -1)
    e = np.stack([o[np.maximum(place[after] - i, 0)] for i in range(4)])
    e = np.take_along_axis(e, np.argsort(rng.random((4, M)), axis=0), axis=0)
    k = np.flatnonzero(place[after] >= M // 2 + 4)[::2]
    a = place[after[k]]
    e[:, k] = o[np.stack([a - M // 2 - 4, a - 1, a, a - 2])]
    return {"x": x.reshape(N, 128, 4 * C).astype(BF), "u": u.reshape(N, 128, 512), "v": d["v"], **still(rng), "sc": stored(e)}
def setup_inputs_huge(rng):
    d = numbers_of(rng)
    g = signs(rng)
    x = 2.0 ** 30 * (0.6 + 0.4 * rng.random((N, 128, 4 * C)))
    u = d["u"].reshape(N, 128, 128, 4)
    a = 2.0 ** 30 * (1 - 0.25 * rng.random((N, 128, 4))) * g[:, None, None]
    u[:, :, 0] = a.astype(np.float32).astype(BF)
    minus, plus = np.flatnonzero(np.repeat(g < 0, C)), np.flatnonzero(np.repeat(g > 0, C))
    e = anywhere(rng)
    k = np.concatenate([rng.permutation(C) % 3 for r in range(N)])
    e[:, k == 0] = minus[e[:, k == 0] % (M // 2)]
    e[:, k == 1] = plus[e[:, k == 1] % (M // 2)]
    return {"x": x.astype(np.float32).astype(BF), "u": u.reshape(N, 128, 512), "v": d["v"], **still(rng), "sc": stored(e)}
def setup_inputs_one(rng):
    d = numbers_of(rng)
    x = d["x"].reshape(N, 128, C, 4)
    u = d["u"].reshape(N, 128, 128, 4)
    w = np.array(f(rng, N, 128, 2048)).reshape(N, 128, 4, 128, 4)
    for i, k in ((0, 2 ** 23), (127, -2 ** 23)):
        x[:, i] = 0
        x[:, i, :, 0] = 4
        u[:, i, 0] = 0
        u[:, i, 0, 0] = k
        w[:, i] = 0
        w[:, i, :, :, 0] = k
    for i in (0, 127):
        w[:, :, :, i] = 0
        w[:, i, 0, i, 0] = 32
    a = C * rng.permutation(N)
    e = a[0] + rng.integers(0, C, (4, M))
    e[:, a[1]:a[1] + C] = a[0] + rng.permutation(C)
    e[:, a[2]:a[2] + C] = e[:, a[2]:a[2] + 1].copy()
    c = a[0] + rng.permutation(C)
    e[:, c[:-1]] = np.roll(c[:-1], -1)
    e[:, c[-1]] = c[-1]
    return {"x": x.reshape(N, 128, 4 * C), "u": u.reshape(N, 128, 512), "v": d["v"], **weights(rng, w.reshape(N, 128, 2048)), "sc": stored(e)}
def setup_inputs_spread(rng):
    d = setup_inputs(rng)
    d["x"] = wide(rng, N, 128, 4 * C, cols=6)
    return d
def check_inputs(d):
    b = []
    for k in ("x", "u", "v"):
        a = np.abs(d[k].astype(np.float32))
        if not (np.isfinite(a).all() and ((a == 0) | (a >= 2.0 ** -30) & (a <= 2.0 ** 30)).all()): b.append("a value of " + k)
    if ((d["sc"] < 0) | (d["sc"] >= M)).any(): b.append("an entry of sc")
    return b
def reference(x, u, v, wc, ws, sc):
    qu = [mx_ref.quantize(u[r]) for r in range(N)]
    lay = [pk(wc[r], ws[r]) for r in range(N)]
    follow = np.concatenate([entries(sc[r]).reshape(4, C) for r in range(N)], axis=1)
    now = [x[r] for r in range(N)]
    for t in range(R):
        q = [mx_ref.quantize(now[r]) for r in range(N)]
        s = np.concatenate([mx_ref.matmul(qu[r], q[r])[0] for r in range(N)]) + np.float32(0.0)
        p = [follow[np.argmax(s[follow], axis=0), np.arange(M)]]
        for g in range(7): p.append(p[g][p[g]])
        p = np.stack(p)
        z = decode(join(*q)).astype(BF)
        z = decode(mx_ref.quantize(z)).astype(BF)
        now = []
        for r in range(N):
            h = mx_ref.quantize(gcols(z, p[:, C * r:C * r + C]))
            now.append(tile([np.maximum(mx_ref.matmul(pick(lay[r], np.arange(128 * b, 128 * b + 128)), h), np.float32(0.0)) * np.float32(0.03125) for b in range(4)]))
    y, pl = np.zeros((N, 128, C), np.float32), np.zeros((N, 8, C), np.float32)
    oc, osc = np.zeros((N, 128, 4 * C), np.uint8), np.zeros((N, 16, C), np.uint8)
    for r in range(N):
        last = mx_ref.quantize(now[r])
        y[r] = mx_ref.matmul(mx_ref.quantize(v[r]), last)
        pl[r] = p[:, C * r:C * r + C]
        oc[r], osc[r] = emit(last)
    return {"y": y, "pl": pl, "oc": oc, "osc": osc}

@@ -1,0 +1,454 @@
+from concourse.bass import DstId, RemoteDMATransfer
+from concourse.mybir import dt, AluOpType as ALU, ActivationFunctionType as AF
+
+N, C, ROUNDS = 4, 384, 2
+SL = 400
+RW = 4 * SL
+F32, BF, I32, U16, CODE, U8 = "float32", "bfloat16", "int32", "uint16", "float8_e4m3fn_x4", "uint8"
+
+SCRATCH = {"ps": ("psum", [128, 4096], F32)}
+
+
+def _sb(name, n, d):
+    SCRATCH[name] = ("sbuf", [128, n], d)
+
+
+for _t in range(3):
+    _sb("xt%d" % _t, 4 * C, BF); _sb("xq%d" % _t, C, CODE); _sb("xs%d" % _t, C, U8)
+for _t in range(ROUNDS):
+    _sb("sh%d" % _t, 4 * C, BF); _sb("pq%d" % _t, C, CODE); _sb("pp%d" % _t, C, U8)
+    _sb("lq%d" % _t, C, CODE); _sb("lp%d" % _t, C, U8)
+    _sb("tab%d" % _t, 4 * RW, BF)
+    _sb("ug%d" % _t, 4 * C, BF); _sb("gq%d" % _t, C, CODE); _sb("gp%d" % _t, C, U8)
+    _sb("mq%d" % _t, 352, CODE); _sb("mp%d" % _t, 352, U8)
+    _sb("ht%d" % _t, 4 * C, BF); _sb("hq%d" % _t, C, CODE); _sb("hp%d" % _t, C, U8)
+    _sb("ssend%d" % _t, 4, F32); _sb("sland%d" % _t, 12, F32)
+for _n in ("u", "v"):
+    _sb(_n + "t", 512, BF); _sb(_n + "q", 128, CODE); _sb(_n + "p", 128, U8)
+for _n, _w, _d in (
+        ("wq", 512, CODE), ("wp", 512, U8), ("et", 2048, BF), ("eq", 512, CODE), ("ep", 512, U8),
+        ("aa", 1536, F32), ("sw", 1536, F32), ("call", 48, F32), ("g0", 768, F32), ("tt", 800, F32), ("lam", 1536, F32),
+        ("rr", 7 * RW, F32), ("gf", C, F32), ("tf", C, F32),
+        ("scraw", 32, I32), ("scl", 48, I32), ("lsc", 48, U16), ("ll0", 100, U16), ("ll1", 100, U16),
+        ("lf", 24, U16), ("ld", 96, U16),
+        ("wk", 256, F32), ("in1", 64, F32), ("yy", 64, F32), ("fs", 64, F32),
+        ("idm", 128, F32), ("ic", 96, F32), ("i96", 96, F32), ("i12", 12, F32),
+        ("pint", 8, I32), ("col", 8, F32), ("bet", 96, F32),
+        ("ysb", C, F32), ("plsend", 24, F32), ("pland", 24, F32), ("in2", 32, F32), ("plt", 32, F32)):
+    _sb(_n, _w, _d)
+
+SEMAPHORES = ["cV", "cS", "cT", "cG", "sent", "scarr", "plarr", "dx", "du", "dsc", "dsh", "dw", "dv", "dpad", "dy", "doc", "dpl"]
+for _t in range(ROUNDS):
+    SEMAPHORES += ["sarr%d" % _t, "dso%d" % _t, "p1arr%d" % _t, "dp1%d" % _t, "drep%d" % _t]
+    SEMAPHORES += ["p2arr%d_%d" % (_t, _k) for _k in range(N)]
+
+
+def _split(topo, cores, r):
+    o = [k for k in range(N) if k != r]
+    e = topo.engines(cores[r], cores[o[0]])
+    h, q = len(e) // 2, len(e) // 4
+    return [(o[0], e[:q], e[h:h + q]), (o[1], e[q:h], e[h + q:]), (o[2], e[h:], e[:h])]
+
+
+def _mask(es):
+    m = 0
+    for e in es:
+        m |= 1 << e
+    return m
+
+
+def rank_program(g, core, T, topo):
+    r = T.rank_of(core)
+    if r is None:
+        return
+    cores = T.cores
+    others = [k for k in range(N) if k != r]
+    queue = {"V": g.vector, "S": g.scalar, "T": g.tensor, "G": g, "Y": g.sync}
+    ops = []
+    total = {}
+    pool = []
+
+    def v(name, c0, c1, step=1, p0=0, p1=128):
+        ap = T[name][p0:p1, c0:c1:step] if step != 1 else T[name][p0:p1, c0:c1]
+        if name == "ps":
+            cols = frozenset(c // 512 for c in range(c0, c1, step))
+            return (ap, (name, 0, 128, cols))
+        return (ap, (name, p0, p1, frozenset(range(c0, c1, step))))
+
+    def u8(x):
+        return (x[0].bitcast(dt.uint8), x[1])
+
+    def add(eng, fn, outs, ins, sem=None, inc=0, after=()):
+        ops.append({"e": eng, "f": fn, "w": [o[1] for o in outs], "r": [i[1] for i in ins], "sem": sem, "a": set(after)})
+        if sem is not None:
+            total[sem] = total.get(sem, 0) + inc
+
+    def arrive(sem, inc, outs):
+        add("X", None, outs, [], sem, inc)
+
+    def dma(eng, out, in_, sem):
+        add(eng, lambda q: q.dma_start(out[0], in_[0]), [out] if out[1] else [], [in_] if in_[1] else [], sem, 16)
+
+    def hbm(ap):
+        return (ap, None)
+
+    def copy(eng, out, in_):
+        if eng == "V":
+            add("V", lambda q: q.tensor_copy(out[0], in_[0]), [out], [in_])
+        else:
+            add("S", lambda q: q.activation(out[0], in_[0], AF.Copy), [out], [in_])
+
+    def gather(eng, out, win, off):
+        if eng == "V":
+            add("V", lambda q: q.tensor_copy(out[0], win[0].indirect(off[0])), [out], [win, off])
+        else:
+            add("S", lambda q: q.activation(out[0], win[0].indirect(off[0]), AF.Copy), [out], [win, off])
+
+    def tt_(out, a, b, op):
+        add("V", lambda q: q.tensor_tensor(out[0], a[0], b[0], op), [out], [a, b])
+
+    def ts(out, a, s1, op0, s2=None, op1=None):
+        ins = [a] + [s for s in (s1, s2) if isinstance(s, tuple)]
+        x1 = s1[0] if isinstance(s1, tuple) else s1
+        x2 = s2[0] if isinstance(s2, tuple) else s2
+        if op1 is None:
+            add("V", lambda q: q.tensor_scalar(out[0], a[0], x1, None, op0), [out], ins)
+        else:
+            add("V", lambda q: q.tensor_scalar(out[0], a[0], x1, x2, op0, op1), [out], ins)
+
+    def tr(out, in_):
+        add("V", lambda q: q.transpose(out[0], in_[0]), [out], [in_])
+
+    def mset(out, val):
+        add("V", lambda q: q.memset(out[0], val), [out], [])
+
+    def iota(out, pat, base, cm, flt=True):
+        p0, p1 = out[1][1], out[1][2]
+        after = [i for i, a, b in pool if a != p0 and a < p1 and p0 < b]
+        pool.append((len(ops), p0, p1))
+        if flt:
+            add("G", lambda q: q.iota(out[0], pat, base, cm, allow_small_or_imprecise_dtypes=True), [out], [], after=after)
+        else:
+            add("G", lambda q: q.iota(out[0], pat, base, cm), [out], [], after=after)
+
+    def quant(qn, sn, tn, n):
+        a, b, c = v(qn, 0, n), v(sn, 0, n), v(tn, 0, 4 * n)
+        add("V", lambda q: q.quantize_mx(a[0], b[0], c[0]), [a, b], [c])
+
+    def mm(bank, lq, lp, l0, rq, rp, r0, n):
+        o = v("ps", 512 * bank, 512 * bank + n)
+        a, b, c, d = v(lq, l0, l0 + 128), v(lp, l0, l0 + 128), v(rq, r0, r0 + n), v(rp, r0, r0 + n)
+        add("T", lambda q: q.matmul_mx(o[0], a[0], b[0], c[0], d[0], True, True), [o], [a, b, c, d])
+
+    def dst(k):
+        rid, pid, _ = topo.addr(cores[k])
+        return DstId(rid=rid, pnc=pid)
+
+    def send_all(src, land, sem):
+        es = topo.engines(core, cores[others[0]])
+        add("G", lambda q: q.remote_dma_fused([RemoteDMATransfer(
+            dst_ids=[dst(k) for k in others], dma_engine_mask=_mask(es), remote_sem=T.sem[sem],
+            srcs=[src[0]], dsts=[land[0] for k in others])], local_sem=T.sem.sent), [], [src], "sent", len(es))
+
+    def n_all(k):
+        return len(topo.engines(cores[k], core))
+
+    def send_each(srcs, lands, which, sem):
+        plan = _split(topo, cores, r)
+        trs = [RemoteDMATransfer(dst_ids=[dst(p[0])], dma_engine_mask=_mask(p[which]), remote_sem=T.sem[sem],
+                                 src=s[0], dst=l[0]) for p, s, l in zip(plan, srcs, lands)]
+        add("G", lambda q: q.remote_dma_fused(trs, local_sem=T.sem.sent), [], srcs, "sent", sum(len(p[which]) for p in plan))
+
+    def send_tiles(sq, sp, lq, lp, place, sem):
+        send_each([u8(v(sq, 96 * k, 96 * k + 96)) for k in others], [u8(v(lq, place(k), place(k) + 96)) for k in others], 1, sem)
+        send_each([v(sp, 96 * k, 96 * k + 96) for k in others], [v(lp, place(k), place(k) + 96) for k in others], 2, sem)
+
+    def n_each(k, which):
+        return [len(p[which]) for p in _split(topo, cores, k) if p[0] == r][0]
+
+    def n_tiles(k):
+        return n_each(k, 1) + n_each(k, 2)
+
+    def p2place(src, at):
+        return (0, 128, 224)[[k for k in range(N) if k != at].index(src)]
+
+    def sgn(q, bit):
+        return -1 if q & bit else 1
+
+    def pads(t):
+        for s in range(4):
+            mset(v("tab%d" % t, 4 * SL * s, 4 * SL * s + 64), 0.0)
+
+    SH, PQ, P16, M1, M2 = [v("col", i, i + 1) for i in range(5)]
+
+    dma("Y", v("xt0", 0, 4 * C), hbm(T.x[:, :]), "dx")
+    dma("S", v("ut", 0, 512), hbm(T.u[:, :]), "du")
+    for q in range(4):
+        for e in range(2):
+            p = 32 * q + 16 * e
+            dma("S", v("scraw", 0, 30, 1, p, p + 16), hbm(T.sc[:, 48 * e + 6 * q:48 * e + 6 * q + 30]), "dsc")
+    for k in range(4):
+        for q in range(4):
+            dma("Y", v("sh0", 384 * k, 384 * k + 384, 1, 32 * q, 32 * q + 32),
+                hbm(T.x[32 * k:32 * k + 32, 384 * q:384 * q + 384]), "dsh")
+    iota(v("ic", 0, 96), [[1, 96]], 0, 0)
+    iota(v("pint", 0, 1), [[0, 1]], 0, 1, False)
+    iota(v("idm", 0, 128), [[-1, 128]], 0, 1)
+    iota(v("i96", 0, 96), [[32, 48], [0, 2]], 0, 1)
+    iota(v("bet", 16, 32), [[96, 16]], 0, 0)
+    iota(v("i12", 0, 12), [[32, 12]], 16, 1)
+    for q in range(4):
+        iota(v("bet", 0, 16, 1, 32 * q, 32 * q + 32), [[96, 4], [sgn(q, 2) * 2 * SL, 2], [sgn(q, 1) * SL, 2]], 16 + SL * q, 0)
+    mset(v("et", 0, 2048), 0.0)
+    mset(v("in1", 0, 64), 0.0)
+    mset(v("in2", 0, 32), 0.0)
+    for i in range(16):
+        copy("S", v("aa", 96 * i, 96 * i + 96), v("ic", 0, 96))
+    for i, m in enumerate((16, 96, 112, 15)):
+        ts(v("pint", 1 + i, 2 + i), v("pint", 0, 1), m, ALU.bitwise_and)
+    ts(v("et", 0, 512, 4), v("idm", 0, 128), 0.0, ALU.is_equal)
+    copy("V", v("col", 0, 3), v("pint", 1, 4))
+    ts(M1, v("pint", 4, 5), 1.0, ALU.is_equal)
+    ts(M2, v("pint", 4, 5), 2.0, ALU.is_equal)
+    for b in range(1, 4):
+        copy("S", v("et", 512 * b + b, 512 * b + 512, 4), v("et", 0, 512, 4))
+    quant("uq", "up", "ut", 128)
+    for kk in range(2):
+        copy("V", v("scl", 12 * r + 6 * kk, 12 * r + 6 * kk + 6), v("scraw", 24 * kk, 24 * kk + 6))
+    send_all(v("scl", 12 * r, 12 * r + 12), v("scl", 12 * r, 12 * r + 12), "scarr")
+    arrive("scarr", sum(n_all(k) for k in others), [v("scl", 12 * k, 12 * k + 12) for k in others])
+
+    def late_setup():
+        dma("Y", u8(v("wq", 0, 512)), hbm(T.wc[:, :]), "dw")
+        dma("Y", v("wp", 0, 512), hbm(T.ws[:, :]), "dw")
+        dma("Y", v("vt", 0, 512), hbm(T.v[:, :]), "dv")
+        for t in range(ROUNDS):
+            for c0 in (96, 320):
+                dma("Y", u8(v("mq%d" % t, c0, c0 + 32)), u8(v("xq0", 0, 32)), "dpad")
+                dma("Y", v("mp%d" % t, c0, c0 + 32), v("xs0", 0, 32), "dpad")
+        copy("V", v("bet", 32, 48, 1, 0, 64), v("bet", 0, 16, 1, 64, 128))
+        copy("V", v("bet", 32, 48, 1, 64, 128), v("bet", 0, 16, 1, 0, 64))
+        tt_(v("bet", 48, 64), v("bet", 16, 32), v("bet", 0, 16), ALU.subtract)
+        ts(v("aa", 1, 1536, 16), v("i96", 0, 96), PQ, ALU.subtract)
+        tt_(v("bet", 64, 80), v("bet", 32, 48), v("bet", 0, 16), ALU.subtract)
+        ts(v("bet", 16, 32), v("bet", 48, 64), M2, ALU.mult)
+        ts(v("lf", 0, 24, 2), v("i12", 0, 12), P16, ALU.subtract)
+        ts(v("bet", 32, 48), v("bet", 64, 80), M1, ALU.mult)
+        tt_(v("bet", 48, 64), v("bet", 16, 32), v("bet", 0, 16), ALU.add)
+        quant("eq", "ep", "et", 512)
+        tt_(v("bet", 80, 96), v("bet", 48, 64), v("bet", 32, 48), ALU.add)
+        for i in range(16):
+            o, a, bi = v("lam", 96 * i, 96 * i + 96), v("ic", 0, 96), v("bet", 80 + i, 81 + i)
+            add("S", lambda q, o=o, a=a, bi=bi: q.activation(o[0], a[0], AF.Identity, bias=bi[0]), [o], [a, bi])
+        for kk in range(2):
+            for d in range(4):
+                copy("V", v("lsc", 24 * kk + 6 * d, 24 * kk + 6 * d + 6), v("scl", 12 * d + 6 * kk, 12 * d + 6 * kk + 6))
+
+    def step(gi, win, lst, last):
+        if last:
+            cuts = (("V", 0, 24), ("S", 40, 100), ("V", 24, 40))
+        elif gi == 0:
+            cuts = (("S", 20, 50), ("V", 0, 20), ("S", 50, 100))
+        else:
+            cuts = (("S", 26, 50), ("V", 0, 26), ("S", 50, 100))
+        for eng, a, b in cuts:
+            gather(eng, v("rr", RW * gi + 16 * a, RW * gi + 16 * b), win, v(lst, a, b))
+
+    def wrap(gi, lst):
+        tr(v("tt", 0, 800), v("rr", RW * gi, RW * gi + 800))
+        ts(v(lst, 0, 50), v("tt", 0, 800, 16), SH, ALU.subtract)
+        for a, b in ((0, 64), (64, 0)):
+            ts(v(lst, 50, 100, 1, a, a + 64), v("tt", 1, 800, 16, b, b + 64), v("col", 0, 1, 1, b, b + 64), ALU.subtract)
+
+    def row(gi):
+        return v("rr", RW * gi, RW * gi + RW)
+
+    for t in range(ROUNDS):
+        s = str(t)
+        X, XQ, XS = "xt" + s, "xq" + s, "xs" + s
+        shuffle = [(q, k) for k in range(4) for q in range(4)] if t else []
+        for q, k in shuffle[:6]:
+            copy("S", v("sh" + s, 384 * k, 384 * k + 384, 1, 32 * q, 32 * q + 32), v(X, 384 * q, 384 * q + 384, 1, 32 * k, 32 * k + 32))
+        quant(XQ, XS, X, C)
+        for i in range(3):
+            mm(i, XQ, XS, 128 * i, "uq", "up", 0, 128)
+        copy("V", v("ssend" + s, 0, 3), v("ps", 0, 1536, 512))
+        send_all(v("ssend" + s, 0, 3), v("sland" + s, 3 * r, 3 * r + 3), "sarr" + s)
+        dma("Y", v("sland" + s, 3 * r, 3 * r + 3), v("ssend" + s, 0, 3), "dso" + s)
+        arrive("sarr" + s, sum(n_all(k) for k in others), [v("sland" + s, 3 * k, 3 * k + 3) for k in others])
+        for q, k in shuffle[6:]:
+            copy("V", v("sh" + s, 384 * k, 384 * k + 384, 1, 32 * q, 32 * q + 32), v(X, 384 * q, 384 * q + 384, 1, 32 * k, 32 * k + 32))
+        quant("pq" + s, "pp" + s, "sh" + s, C)
+        send_tiles("pq" + s, "pp" + s, "lq" + s, "lp" + s, lambda k: 96 * r, "p1arr" + s)
+        dma("Y", u8(v("lq" + s, 96 * r, 96 * r + 96)), u8(v("pq" + s, 96 * r, 96 * r + 96)), "dp1" + s)
+        dma("Y", v("lp" + s, 96 * r, 96 * r + 96), v("pp" + s, 96 * r, 96 * r + 96), "dp1" + s)
+        arrive("p1arr" + s, sum(n_tiles(k) for k in others),
+               [v(n + s, 96 * k, 96 * k + 96) for k in others for n in ("lq", "lp")])
+        if t == 0:
+            late_setup()
+        pads(t)
+        for q in range(4):
+            for a in range(4):
+                copy("VS"[a % 2], v("call", a, 48, 4, 32 * q, 32 * q + 32), v("sland" + s, 0, 12, 1, 32 * a, 32 * a + 32))
+        copy("V", v("aa", 0, 1536, 32), v("call", 0, 48))
+        copy("S", v("aa", 16, 1536, 32), v("call", 0, 48))
+        tr(v("sw", 0, 1536), v("aa", 0, 1536))
+        gather("V", v("g0", 0, 384), v("sw", 0, 1536), v("lsc", 0, 24))
+        gather("S", v("g0", 384, 768), v("sw", 0, 1536), v("lsc", 24, 48))
+        tr(v("tt", 0, 768), v("g0", 0, 768))
+        TAB = "tab" + s
+        for b in range(4):
+            mm(4 + b, "eq", "ep", 128 * b, "lq" + s, "lp" + s, 0, C)
+        for b in range(4):
+            copy("S", v(TAB, 64 + b, 64 + 4 * C, 4), v("ps", 512 * (4 + b), 512 * (4 + b) + C))
+        for a, b in ((0, 64), (64, 0)):
+            dma("Y", v(TAB, 8 * SL + 64, 12 * SL, 1, a, a + 64), v(TAB, 64, 4 * SL, 1, b, b + 64), "drep" + s)
+        for x in (1, 3):
+            for q in range(4):
+                dma("Y", v(TAB, 4 * SL * x + 64, 4 * SL * (x + 1), 1, 32 * q, 32 * q + 32),
+                    v(TAB, 64, 4 * SL, 1, 32 * (q ^ x), 32 * (q ^ x) + 32), "drep" + s)
+        S0, S1, N0, N1 = v("tt", 0, 384, 16), v("tt", 384, 768, 16), v("tt", 1, 384, 16), v("tt", 385, 768, 16)
+        w = lambda i, a=0, st=1: v("wk", 24 * i + a, 24 * i + 24, st)
+        tt_(w(0), S1, S0, ALU.max)
+        tt_(w(1), S1, S0, ALU.is_gt)
+        tt_(w(2), S1, S0, ALU.is_le)
+        tt_(w(5, 1, 2), w(0, 1, 2), w(0, 0, 2), ALU.is_gt)
+        tt_(w(3), w(1), N1, ALU.mult)
+        tt_(w(4), w(2), N0, ALU.mult)
+        tt_(w(5, 0, 2), w(0, 1, 2), w(0, 0, 2), ALU.is_le)
+        tt_(w(6), w(3), w(4), ALU.add)
+        tt_(w(7), w(6), w(5), ALU.mult)
+        for o in (v("in1", 1, 13), v("in1", 32, 44), v("fs", 1, 25, 2)):
+            tt_(o, w(7, 0, 2), w(7, 1, 2), ALU.add)
+        tr(v("yy", 0, 64), v("in1", 0, 64))
+        tr(v("fs", 0, 64, 2), v("yy", 16, 48))
+        for x in (1, 0, 2, 3):
+            n = (128, 32, 64, 32)[x]
+            for p in range(0, 128, n):
+                o = p ^ (32 * x)
+                copy("V", v("ll0", 25 * x, 25 * x + 25, 1, p, p + n), v("fs", 0, 25, 1, o, o + n))
+        g0 = 2 * r
+        step(0, v("lam", 0, 1536), "ll0", g0 == 0)
+        for gi in range(g0):
+            lst = "ll%d" % ((gi + 1) % 2)
+            wrap(gi, lst)
+            step(gi + 1, row(gi), lst, gi + 1 == g0)
+        tr(v("tt", 0, 384), v("rr", RW * g0, RW * g0 + 384))
+        ts(v("lf", 1, 24, 2), v("tt", 16, 384, 32), SH, ALU.subtract)
+        gather("V", v("gf", 0, 192), row(g0), v("lf", 0, 12))
+        gather("S", v("gf", 192, 384), row(g0), v("lf", 12, 24))
+        tr(v("tf", 0, 384), v("gf", 0, 384))
+        for b in (2, 3, 0, 1):
+            ts(v("ld", 24 * b, 24 * b + 24), v("tf", 0, 384, 16), 4.0, ALU.mult, float(b), ALU.add)
+        for b in (2, 0, 3, 1):
+            gather("VVSS"[b], v("ug" + s, b, 4 * C, 4), v(TAB, 0, 4 * RW), v("ld", 24 * b, 24 * b + 24))
+        quant("gq" + s, "gp" + s, "ug" + s, C)
+        send_tiles("gq" + s, "gp" + s, "mq" + s, "mp" + s, lambda k: p2place(r, k), "p2arr%d_%d" % (t, r))
+        for k in others:
+            c0 = p2place(k, r)
+            arrive("p2arr%d_%d" % (t, k), n_tiles(k), [v(n + s, c0, c0 + 96) for n in ("mq", "mp")])
+        if t == 0:
+            quant("vq", "vp", "vt", 128)
+        else:
+            copy("S", v("plsend", 0, 24), v("tf", 2, 384, 16))
+            send_each([v("plsend", 6 * k, 6 * k + 6) for k in others], [v("pland", 6 * r, 6 * r + 6) for k in others], 2, "plarr")
+            arrive("plarr", sum(n_each(k, 2) for k in others), [v("pland", 6 * k, 6 * k + 6) for k in others])
+        H = "ht" + s
+        for i, k in enumerate([r] + others):
+            if k == r:
+                names, c0 = ("gq" + s, "gp" + s), 96 * r
+                lo = min(c0, C - 128)
+            else:
+                names, c0 = ("mq" + s, "mp" + s), p2place(k, r)
+                lo = 96 if c0 == 128 else c0
+            base = 4 * (i % 2)
+            for b in (0, 2, 1, 3):
+                mm(base + b, "eq", "ep", 128 * b, names[0], names[1], lo, 128)
+            for b in (0, 2, 1, 3):
+                for q in range(4):
+                    c = 512 * (base + b) + c0 - lo
+                    copy("VVSS"[b], v(H, 384 * q + b, 384 * q + 384, 4, 32 * k, 32 * k + 32), v("ps", c, c + 96, 1, 32 * q, 32 * q + 32))
+        quant("hq" + s, "hp" + s, H, C)
+        XN = "xt%d" % (t + 1)
+        for b in (0, 2, 1, 3):
+            mm(b, "wq", "wp", 128 * b, "hq" + s, "hp" + s, 0, C)
+        for b in (0, 2, 1, 3):
+            o, a = v(XN, b, 4 * C, 4), v("ps", 512 * b, 512 * b + C)
+            if b < 2:
+                ts(o, a, 0.0, ALU.max, 0.03125, ALU.mult)
+            else:
+                add("S", lambda q, o=o, a=a: q.activation(o[0], a[0], AF.Relu, scale=0.03125), [o], [a])
+
+    quant("xq2", "xs2", "xt2", C)
+    mm(4, "vq", "vp", 0, "xq2", "xs2", 0, C)
+    dma("Y", hbm(T.oc[:, :]), u8(v("xq2", 0, C)), "doc")
+    for k in range(4):
+        dma("S", hbm(T.osc[4 * k:4 * k + 4, :]), v("xs2", 0, C, 1, 32 * k, 32 * k + 4), "doc")
+    copy("V", v("in2", 6 * r, 6 * r + 6), v("plsend", 6 * r, 6 * r + 6))
+    for a, b in ((0, 6 * r), (6 * r + 6, 24)):
+        if a < b:
+            copy("V", v("in2", a, b), v("pland", a, b))
+    copy("V", v("ysb", 0, C), v("ps", 2048, 2048 + C))
+    dma("Y", hbm(T.y[:, :]), v("ysb", 0, C), "dy")
+    tr(v("plt", 0, 32), v("in2", 0, 32))
+    for q in range(4):
+        for e in range(2):
+            dma("YS"[e], hbm(T.pl[e:8:2, 96 * q:96 * q + 96]), v("plt", 16 * e, 16 * e + 16, 1, 32 * q, 32 * q + 24), "dpl")
+
+    def meet(a, b):
+        return a[0] == b[0] and a[1] < b[2] and b[1] < a[2] and not a[3].isdisjoint(b[3])
+
+    seen = {}
+    for i, op in enumerate(ops):
+        deps = set(op["a"])
+        for regs, mine in ((op["w"], True), (op["r"], False)):
+            for reg in regs:
+                for j, other, wrote in seen.get(reg[0], []):
+                    if ops[j]["e"] == "G" and ops[j]["sem"] is not None:
+                        continue
+                    clash = mine or wrote or (reg[0] == "ps" and ops[j]["e"] != op["e"])
+                    if clash and j != i and meet(reg, other):
+                        deps.add(j)
+        op["d"] = set() if op["e"] == "X" else deps
+        for reg in op["w"]:
+            seen.setdefault(reg[0], []).append((i, reg, True))
+        for reg in op["r"]:
+            seen.setdefault(reg[0], []).append((i, reg, False))
+    need = set()
+    for op in ops:
+        last = {}
+        for j in op["d"]:
+            if ops[j]["sem"] is None:
+                last[ops[j]["e"]] = max(last.get(ops[j]["e"], -1), j)
+        op["last"] = last
+        need.update(last.values())
+    count = {}
+    for i, op in enumerate(ops):
+        if op["sem"] is None and i in need:
+            count[op["e"]] = count.get(op["e"], 0) + 1
+            op["n"] = count[op["e"]]
+    waited = {}
+    for i, op in enumerate(ops):
+        if op["e"] == "X":
+            continue
+        q = queue[op["e"]]
+        want = {}
+        for e, j in op["last"].items():
+            want["c" + e] = ops[j]["n"]
+        for j in op["d"]:
+            if ops[j]["sem"] is not None:
+                want[ops[j]["sem"]] = total[ops[j]["sem"]]
+        for name in sorted(want):
+            if waited.get((op["e"], name), 0) < want[name]:
+                q.wait_ge(T.sem[name], want[name])
+                waited[(op["e"], name)] = want[name]
+        ins = op["f"](q)
+        if op["sem"] is None:
+            if "n" in op:
+                ins.then_inc(T.sem["c" + op["e"]], 1)
+        elif op["sem"] != "sent":
+            ins.then_inc(T.sem[op["sem"]], 16)
+    for e, n in sorted(count.items()):
+        g.wait_ge(T.sem["c" + e], n)
+    for name in sorted(total):
+        g.wait_ge(T.sem[name], total[name])

@@ -2,8 +2,10 @@ from concourse.bass import DstId, RemoteDMATransfer
 from concourse.mybir import dt, AluOpType as ALU, ActivationFunctionType as AF
 
 N, C, ROUNDS = 4, 384, 2
+HC = C // 2
 SL = 400
 RW = 4 * SL
+BIG = 1e29
 F32, BF, I32, U16, CODE, U8 = "float32", "bfloat16", "int32", "uint16", "float8_e4m3fn_x4", "uint8"
 
 SCRATCH = {"ps": ("psum", [128, 4096], F32)}
@@ -20,6 +22,7 @@ for _t in range(ROUNDS):
     _sb("lq%d" % _t, C, CODE); _sb("lp%d" % _t, C, U8)
     _sb("tab%d" % _t, 4 * RW, BF)
     _sb("ug%d" % _t, 4 * C, BF); _sb("gq%d" % _t, C, CODE); _sb("gp%d" % _t, C, U8)
+    _sb("oq%d" % _t, 128, CODE); _sb("op%d" % _t, 128, U8)
     _sb("mq%d" % _t, 352, CODE); _sb("mp%d" % _t, 352, U8)
     _sb("ht%d" % _t, 4 * C, BF); _sb("hq%d" % _t, C, CODE); _sb("hp%d" % _t, C, U8)
     _sb("ssend%d" % _t, 4, F32); _sb("sland%d" % _t, 12, F32)
@@ -29,9 +32,9 @@ for _n, _w, _d in (
         ("wq", 512, CODE), ("wp", 512, U8), ("et", 2048, BF), ("eq", 512, CODE), ("ep", 512, U8),
         ("aa", 1536, F32), ("sw", 1536, F32), ("call", 48, F32), ("g0", 768, F32), ("tt", 800, F32), ("lam", 1536, F32),
         ("rr", 7 * RW, F32), ("gf", C, F32), ("tf", C, F32),
-        ("scraw", 32, I32), ("scl", 48, I32), ("lsc", 48, U16), ("ll0", 100, U16), ("ll1", 100, U16),
+        ("scraw", 56, I32), ("scl", 48, I32), ("lsc", 48, U16), ("ll0", 100, U16), ("ll1", 100, U16),
         ("lf", 24, U16), ("ld", 96, U16),
-        ("wk", 256, F32), ("in1", 64, F32), ("yy", 64, F32), ("fs", 64, F32),
+        ("wk", 320, F32), ("so", 136, F32), ("yy", 64, F32), ("fs", 64, F32),
         ("idm", 128, F32), ("ic", 96, F32), ("i96", 96, F32), ("i12", 12, F32),
         ("pint", 8, I32), ("col", 8, F32), ("bet", 96, F32),
         ("ysb", C, F32), ("plsend", 24, F32), ("pland", 24, F32), ("in2", 32, F32), ("plt", 32, F32)):
@@ -39,7 +42,7 @@ for _n, _w, _d in (
 
 SEMAPHORES = ["cV", "cS", "cT", "cG", "sent", "scarr", "plarr", "dx", "du", "dsc", "dsh", "dw", "dv", "dpad", "dy", "doc", "dpl"]
 for _t in range(ROUNDS):
-    SEMAPHORES += ["sarr%d" % _t, "dso%d" % _t, "p1arr%d" % _t, "dp1%d" % _t, "drep%d" % _t]
+    SEMAPHORES += ["sarr%d" % _t, "p1arr%d" % _t, "dp1%d" % _t, "drep%d" % _t]
     SEMAPHORES += ["p2arr%d_%d" % (_t, _k) for _k in range(N)]
 
 
@@ -107,6 +110,9 @@ def rank_program(g, core, T, topo):
     def tt_(out, a, b, op):
         add("V", lambda q: q.tensor_tensor(out[0], a[0], b[0], op), [out], [a, b])
 
+    def scan(out, a, b, first, op0, op1):
+        add("V", lambda q: q.tensor_tensor_scan(out[0], a[0], b[0], first, op0, op1), [out], [a, b])
+
     def ts(out, a, s1, op0, s2=None, op1=None):
         ins = [a] + [s for s in (s1, s2) if isinstance(s, tuple)]
         x1 = s1[0] if isinstance(s1, tuple) else s1
@@ -131,8 +137,8 @@ def rank_program(g, core, T, topo):
         else:
             add("G", lambda q: q.iota(out[0], pat, base, cm), [out], [], after=after)
 
-    def quant(qn, sn, tn, n):
-        a, b, c = v(qn, 0, n), v(sn, 0, n), v(tn, 0, 4 * n)
+    def quant(qn, sn, tn, n, c0=0, o0=0):
+        a, b, c = v(qn, o0, o0 + n), v(sn, o0, o0 + n), v(tn, 4 * c0, 4 * (c0 + n))
         add("V", lambda q: q.quantize_mx(a[0], b[0], c[0]), [a, b], [c])
 
     def mm(bank, lq, lp, l0, rq, rp, r0, n):
@@ -182,11 +188,11 @@ def rank_program(g, core, T, topo):
     SH, PQ, P16, M1, M2 = [v("col", i, i + 1) for i in range(5)]
 
     dma("Y", v("xt0", 0, 4 * C), hbm(T.x[:, :]), "dx")
-    dma("S", v("ut", 0, 512), hbm(T.u[:, :]), "du")
+    dma("Y", v("ut", 0, 512), hbm(T.u[:, :]), "du")
     for q in range(4):
         for e in range(2):
             p = 32 * q + 16 * e
-            dma("S", v("scraw", 0, 30, 1, p, p + 16), hbm(T.sc[:, 48 * e + 6 * q:48 * e + 6 * q + 30]), "dsc")
+            dma("S", v("scraw", 0, 54, 1, p, p + 16), hbm(T.sc[:, 24 * e + 6 * q:24 * e + 6 * q + 54]), "dsc")
     for k in range(4):
         for q in range(4):
             dma("Y", v("sh0", 384 * k, 384 * k + 384, 1, 32 * q, 32 * q + 32),
@@ -194,31 +200,31 @@ def rank_program(g, core, T, topo):
     iota(v("ic", 0, 96), [[1, 96]], 0, 0)
     iota(v("pint", 0, 1), [[0, 1]], 0, 1, False)
     iota(v("idm", 0, 128), [[-1, 128]], 0, 1)
-    iota(v("i96", 0, 96), [[32, 48], [0, 2]], 0, 1)
-    iota(v("bet", 16, 32), [[96, 16]], 0, 0)
-    iota(v("i12", 0, 12), [[32, 12]], 16, 1)
     for q in range(4):
         iota(v("bet", 0, 16, 1, 32 * q, 32 * q + 32), [[96, 4], [sgn(q, 2) * 2 * SL, 2], [sgn(q, 1) * SL, 2]], 16 + SL * q, 0)
     mset(v("et", 0, 2048), 0.0)
-    mset(v("in1", 0, 64), 0.0)
-    mset(v("in2", 0, 32), 0.0)
+    mset(v("so", 0, 136), 0.0)
+    mset(v("wk", 0, 1), -BIG)
+    mset(v("wk", 67, 112, 4), -BIG)
+    for i in range(3):
+        mset(v("wk", 64 + i, 112, 4), BIG)
     for i in range(16):
         copy("S", v("aa", 96 * i, 96 * i + 96), v("ic", 0, 96))
     for i, m in enumerate((16, 96, 112, 15)):
         ts(v("pint", 1 + i, 2 + i), v("pint", 0, 1), m, ALU.bitwise_and)
     ts(v("et", 0, 512, 4), v("idm", 0, 128), 0.0, ALU.is_equal)
-    copy("V", v("col", 0, 3), v("pint", 1, 4))
-    ts(M1, v("pint", 4, 5), 1.0, ALU.is_equal)
-    ts(M2, v("pint", 4, 5), 2.0, ALU.is_equal)
     for b in range(1, 4):
         copy("S", v("et", 512 * b + b, 512 * b + 512, 4), v("et", 0, 512, 4))
-    quant("uq", "up", "ut", 128)
     for kk in range(2):
-        copy("V", v("scl", 12 * r + 6 * kk, 12 * r + 6 * kk + 6), v("scraw", 24 * kk, 24 * kk + 6))
+        for h in range(2):
+            copy("V", v("scl", 12 * r + 2 * kk + h, 12 * r + 12, 4), v("scraw", 48 * kk + h, 48 * kk + 6, 2))
     send_all(v("scl", 12 * r, 12 * r + 12), v("scl", 12 * r, 12 * r + 12), "scarr")
     arrive("scarr", sum(n_all(k) for k in others), [v("scl", 12 * k, 12 * k + 12) for k in others])
+    iota(v("bet", 16, 32), [[96, 16]], 0, 0)
+    iota(v("i96", 0, 96), [[32, 48], [0, 2]], 0, 1)
+    iota(v("i12", 0, 12), [[32, 12]], 16, 1)
 
-    def late_setup():
+    def late_loads():
         dma("Y", u8(v("wq", 0, 512)), hbm(T.wc[:, :]), "dw")
         dma("Y", v("wp", 0, 512), hbm(T.ws[:, :]), "dw")
         dma("Y", v("vt", 0, 512), hbm(T.v[:, :]), "dv")
@@ -226,6 +232,11 @@ def rank_program(g, core, T, topo):
             for c0 in (96, 320):
                 dma("Y", u8(v("mq%d" % t, c0, c0 + 32)), u8(v("xq0", 0, 32)), "dpad")
                 dma("Y", v("mp%d" % t, c0, c0 + 32), v("xs0", 0, 32), "dpad")
+
+    def late_setup():
+        copy("V", v("col", 0, 3), v("pint", 1, 4))
+        ts(M1, v("pint", 4, 5), 1.0, ALU.is_equal)
+        ts(M2, v("pint", 4, 5), 2.0, ALU.is_equal)
         copy("V", v("bet", 32, 48, 1, 0, 64), v("bet", 0, 16, 1, 64, 128))
         copy("V", v("bet", 32, 48, 1, 64, 128), v("bet", 0, 16, 1, 0, 64))
         tt_(v("bet", 48, 64), v("bet", 16, 32), v("bet", 0, 16), ALU.subtract)
@@ -237,12 +248,19 @@ def rank_program(g, core, T, topo):
         tt_(v("bet", 48, 64), v("bet", 16, 32), v("bet", 0, 16), ALU.add)
         quant("eq", "ep", "et", 512)
         tt_(v("bet", 80, 96), v("bet", 48, 64), v("bet", 32, 48), ALU.add)
+
+    def places():
         for i in range(16):
             o, a, bi = v("lam", 96 * i, 96 * i + 96), v("ic", 0, 96), v("bet", 80 + i, 81 + i)
             add("S", lambda q, o=o, a=a, bi=bi: q.activation(o[0], a[0], AF.Identity, bias=bi[0]), [o], [a, bi])
-        for kk in range(2):
-            for d in range(4):
-                copy("V", v("lsc", 24 * kk + 6 * d, 24 * kk + 6 * d + 6), v("scl", 12 * d + 6 * kk, 12 * d + 6 * kk + 6))
+
+    def score_rows(src, m0, m1, s0, engs):
+        for q in range(4):
+            for a in range(4):
+                copy(engs[a % 2], v("call", 4 * m0 + a, 4 * m1, 4, 32 * q, 32 * q + 32), v(src, s0, s0 + m1 - m0, 1, 32 * a, 32 * a + 32))
+        copy(engs[0], v("aa", 128 * m0, 128 * m1, 32), v("call", 4 * m0, 4 * m1))
+        copy(engs[1], v("aa", 128 * m0 + 16, 128 * m1, 32), v("call", 4 * m0, 4 * m1))
+        return v("sw", 128 * m0, 128 * m1), v("aa", 128 * m0, 128 * m1)
 
     def step(gi, win, lst, last):
         if last:
@@ -250,7 +268,7 @@ def rank_program(g, core, T, topo):
         elif gi == 0:
             cuts = (("S", 20, 50), ("V", 0, 20), ("S", 50, 100))
         else:
-            cuts = (("S", 26, 50), ("V", 0, 26), ("S", 50, 100))
+            cuts = (("S", 24, 50), ("V", 0, 24), ("S", 50, 100))
         for eng, a, b in cuts:
             gather(eng, v("rr", RW * gi + 16 * a, RW * gi + 16 * b), win, v(lst, a, b))
 
@@ -263,36 +281,39 @@ def rank_program(g, core, T, topo):
     def row(gi):
         return v("rr", RW * gi, RW * gi + RW)
 
+    quant("xq0", "xs0", "xt0", C)
+    quant("uq", "up", "ut", 128)
     for t in range(ROUNDS):
         s = str(t)
         X, XQ, XS = "xt" + s, "xq" + s, "xs" + s
         shuffle = [(q, k) for k in range(4) for q in range(4)] if t else []
-        for q, k in shuffle[:6]:
+        for q, k in shuffle[:5]:
             copy("S", v("sh" + s, 384 * k, 384 * k + 384, 1, 32 * q, 32 * q + 32), v(X, 384 * q, 384 * q + 384, 1, 32 * k, 32 * k + 32))
-        quant(XQ, XS, X, C)
         for i in range(3):
             mm(i, XQ, XS, 128 * i, "uq", "up", 0, 128)
         copy("V", v("ssend" + s, 0, 3), v("ps", 0, 1536, 512))
         send_all(v("ssend" + s, 0, 3), v("sland" + s, 3 * r, 3 * r + 3), "sarr" + s)
-        dma("Y", v("sland" + s, 3 * r, 3 * r + 3), v("ssend" + s, 0, 3), "dso" + s)
         arrive("sarr" + s, sum(n_all(k) for k in others), [v("sland" + s, 3 * k, 3 * k + 3) for k in others])
-        for q, k in shuffle[6:]:
+        for q, k in shuffle[5:]:
             copy("V", v("sh" + s, 384 * k, 384 * k + 384, 1, 32 * q, 32 * q + 32), v(X, 384 * q, 384 * q + 384, 1, 32 * k, 32 * k + 32))
+        if t == 0:
+            late_setup()
+        own = score_rows("ssend" + s, 3 * r, 3 * r + 3, 0, "SS")
         quant("pq" + s, "pp" + s, "sh" + s, C)
         send_tiles("pq" + s, "pp" + s, "lq" + s, "lp" + s, lambda k: 96 * r, "p1arr" + s)
         dma("Y", u8(v("lq" + s, 96 * r, 96 * r + 96)), u8(v("pq" + s, 96 * r, 96 * r + 96)), "dp1" + s)
         dma("Y", v("lp" + s, 96 * r, 96 * r + 96), v("pp" + s, 96 * r, 96 * r + 96), "dp1" + s)
         arrive("p1arr" + s, sum(n_tiles(k) for k in others),
                [v(n + s, 96 * k, 96 * k + 96) for k in others for n in ("lq", "lp")])
-        if t == 0:
-            late_setup()
         pads(t)
-        for q in range(4):
-            for a in range(4):
-                copy("VS"[a % 2], v("call", a, 48, 4, 32 * q, 32 * q + 32), v("sland" + s, 0, 12, 1, 32 * a, 32 * a + 32))
-        copy("V", v("aa", 0, 1536, 32), v("call", 0, 48))
-        copy("S", v("aa", 16, 1536, 32), v("call", 0, 48))
-        tr(v("sw", 0, 1536), v("aa", 0, 1536))
+        tr(*own)
+        if t == 0:
+            copy("V", v("lsc", 0, 48), v("scl", 0, 48))
+        for m0, m1 in ((0, 3 * r), (3 * r + 3, 12)):
+            if m0 < m1:
+                tr(*score_rows("sland" + s, m0, m1, m0, "VS"))
+        if t == 0:
+            places()
         gather("V", v("g0", 0, 384), v("sw", 0, 1536), v("lsc", 0, 24))
         gather("S", v("g0", 384, 768), v("sw", 0, 1536), v("lsc", 24, 48))
         tr(v("tt", 0, 768), v("g0", 0, 768))
@@ -307,20 +328,17 @@ def rank_program(g, core, T, topo):
             for q in range(4):
                 dma("Y", v(TAB, 4 * SL * x + 64, 4 * SL * (x + 1), 1, 32 * q, 32 * q + 32),
                     v(TAB, 64, 4 * SL, 1, 32 * (q ^ x), 32 * (q ^ x) + 32), "drep" + s)
-        S0, S1, N0, N1 = v("tt", 0, 384, 16), v("tt", 384, 768, 16), v("tt", 1, 384, 16), v("tt", 385, 768, 16)
-        w = lambda i, a=0, st=1: v("wk", 24 * i + a, 24 * i + 24, st)
-        tt_(w(0), S1, S0, ALU.max)
-        tt_(w(1), S1, S0, ALU.is_gt)
-        tt_(w(2), S1, S0, ALU.is_le)
-        tt_(w(5, 1, 2), w(0, 1, 2), w(0, 0, 2), ALU.is_gt)
-        tt_(w(3), w(1), N1, ALU.mult)
-        tt_(w(4), w(2), N0, ALU.mult)
-        tt_(w(5, 0, 2), w(0, 1, 2), w(0, 0, 2), ALU.is_le)
-        tt_(w(6), w(3), w(4), ALU.add)
-        tt_(w(7), w(6), w(5), ALU.mult)
-        for o in (v("in1", 1, 13), v("in1", 32, 44), v("fs", 1, 25, 2)):
-            tt_(o, w(7, 0, 2), w(7, 1, 2), ALU.add)
-        tr(v("yy", 0, 64), v("in1", 0, 64))
+        if t == 0:
+            late_loads()
+        SC, NB = v("tt", 0, 768, 16), v("tt", 1, 768, 16)
+        scan(v("wk", 1, 49), SC, v("wk", 64, 112), -BIG, ALU.max, ALU.min)
+        tt_(v("wk", 192, 240), SC, v("wk", 0, 48), ALU.is_gt)
+        tt_(v("wk", 128, 176), SC, v("wk", 0, 48), ALU.is_le)
+        tt_(v("wk", 256, 304), v("wk", 192, 240), NB, ALU.mult)
+        scan(v("so", 4, 52), v("wk", 128, 176), v("wk", 256, 304), 0.0, ALU.mult, ALU.add)
+        tr(v("yy", 0, 32), v("so", 3, 131, 4))
+        tr(v("yy", 32, 64), v("so", 7, 135, 4))
+        copy("V", v("fs", 1, 25, 2), v("so", 7, 52, 4))
         tr(v("fs", 0, 64, 2), v("yy", 16, 48))
         for x in (1, 0, 2, 3):
             n = (128, 32, 64, 32)[x]
@@ -338,58 +356,70 @@ def rank_program(g, core, T, topo):
         gather("V", v("gf", 0, 192), row(g0), v("lf", 0, 12))
         gather("S", v("gf", 192, 384), row(g0), v("lf", 12, 24))
         tr(v("tf", 0, 384), v("gf", 0, 384))
-        for b in (2, 3, 0, 1):
-            ts(v("ld", 24 * b, 24 * b + 24), v("tf", 0, 384, 16), 4.0, ALU.mult, float(b), ALU.add)
         for b in (2, 0, 3, 1):
-            gather("VVSS"[b], v("ug" + s, b, 4 * C, 4), v(TAB, 0, 4 * RW), v("ld", 24 * b, 24 * b + 24))
-        quant("gq" + s, "gp" + s, "ug" + s, C)
+            ts(v("ld", 24 * b, 24 * b + 24), v("tf", 0, 384, 16), 4.0, ALU.mult, float(b), ALU.add)
+        n1 = 18 if r == N - 1 else 24
+        for b in (2, 0, 3, 1):
+            gather("VVSS"[b], v("ug" + s, b, 64 * n1, 4), v(TAB, 0, 4 * RW), v("ld", 24 * b, 24 * b + n1))
+        quant("gq" + s, "gp" + s, "ug" + s, 16 * n1)
         send_tiles("gq" + s, "gp" + s, "mq" + s, "mp" + s, lambda k: p2place(r, k), "p2arr%d_%d" % (t, r))
         for k in others:
             c0 = p2place(k, r)
             arrive("p2arr%d_%d" % (t, k), n_tiles(k), [v(n + s, c0, c0 + 96) for n in ("mq", "mp")])
+        if n1 < 24:
+            for b in (2, 3, 0, 1):
+                gather("VSSS"[b], v("ug" + s, 64 * n1 + b, 4 * C, 4), v(TAB, 0, 4 * RW), v("ld", 24 * b + n1, 24 * b + 24))
+            quant("oq" + s, "op" + s, "ug" + s, 128, C - 128)
         if t == 0:
             quant("vq", "vp", "vt", 128)
+            mset(v("in2", 0, 32), 0.0)
         else:
             copy("S", v("plsend", 0, 24), v("tf", 2, 384, 16))
             send_each([v("plsend", 6 * k, 6 * k + 6) for k in others], [v("pland", 6 * r, 6 * r + 6) for k in others], 2, "plarr")
             arrive("plarr", sum(n_each(k, 2) for k in others), [v("pland", 6 * k, 6 * k + 6) for k in others])
-        H = "ht" + s
-        for i, k in enumerate([r] + others):
-            if k == r:
-                names, c0 = ("gq" + s, "gp" + s), 96 * r
-                lo = min(c0, C - 128)
-            else:
+        H, HQ, HP = "ht" + s, "hq" + s, "hp" + s
+        XN, XQN, XSN = "xt%d" % (t + 1), "xq%d" % (t + 1), "xs%d" % (t + 1)
+        for i, k in enumerate([r] + others if n1 == 24 else others + [r]):
+            if k != r:
                 names, c0 = ("mq" + s, "mp" + s), p2place(k, r)
                 lo = 96 if c0 == 128 else c0
+            elif n1 == 24:
+                names, c0, lo = ("gq" + s, "gp" + s), 96 * r, 96 * r
+            else:
+                names, c0, lo = ("oq" + s, "op" + s), 32, 0
             base = 4 * (i % 2)
             for b in (0, 2, 1, 3):
                 mm(base + b, "eq", "ep", 128 * b, names[0], names[1], lo, 128)
+            for h in range(2):
+                for b in (0, 2, 1, 3):
+                    for q in (2 * h, 2 * h + 1):
+                        c = 512 * (base + b) + c0 - lo
+                        copy("VVSS"[b], v(H, 384 * q + b, 384 * q + 384, 4, 32 * k, 32 * k + 32), v("ps", c, c + 96, 1, 32 * q, 32 * q + 32))
+                if i == N - 1:
+                    quant(HQ, HP, H, HC, HC * h, HC * h)
+                    for b in (0, 2, 1, 3):
+                        mm(4 * h + b, "wq", "wp", 128 * b, HQ, HP, HC * h, HC)
+        for h in range(2):
             for b in (0, 2, 1, 3):
-                for q in range(4):
-                    c = 512 * (base + b) + c0 - lo
-                    copy("VVSS"[b], v(H, 384 * q + b, 384 * q + 384, 4, 32 * k, 32 * k + 32), v("ps", c, c + 96, 1, 32 * q, 32 * q + 32))
-        quant("hq" + s, "hp" + s, H, C)
-        XN = "xt%d" % (t + 1)
-        for b in (0, 2, 1, 3):
-            mm(b, "wq", "wp", 128 * b, "hq" + s, "hp" + s, 0, C)
-        for b in (0, 2, 1, 3):
-            o, a = v(XN, b, 4 * C, 4), v("ps", 512 * b, 512 * b + C)
-            if b < 2:
-                ts(o, a, 0.0, ALU.max, 0.03125, ALU.mult)
-            else:
-                add("S", lambda q, o=o, a=a: q.activation(o[0], a[0], AF.Relu, scale=0.03125), [o], [a])
+                o, a = v(XN, 4 * HC * h + b, 4 * HC * (h + 1), 4), v("ps", 512 * (4 * h + b), 512 * (4 * h + b) + HC)
+                if b < 2:
+                    ts(o, a, 0.0, ALU.max, 0.03125, ALU.mult)
+                else:
+                    add("S", lambda q, o=o, a=a: q.activation(o[0], a[0], AF.Relu, scale=0.03125), [o], [a])
+            quant(XQN, XSN, XN, HC, HC * h, HC * h)
 
-    quant("xq2", "xs2", "xt2", C)
-    mm(4, "vq", "vp", 0, "xq2", "xs2", 0, C)
+    for h in range(2):
+        mm(h, "vq", "vp", 0, "xq2", "xs2", HC * h, HC)
+    copy("S", v("ysb", 0, HC), v("ps", 0, HC))
     dma("Y", hbm(T.oc[:, :]), u8(v("xq2", 0, C)), "doc")
+    copy("V", v("ysb", HC, C), v("ps", 512, 512 + HC))
+    dma("Y", hbm(T.y[:, :]), v("ysb", 0, C), "dy")
     for k in range(4):
         dma("S", hbm(T.osc[4 * k:4 * k + 4, :]), v("xs2", 0, C, 1, 32 * k, 32 * k + 4), "doc")
     copy("V", v("in2", 6 * r, 6 * r + 6), v("plsend", 6 * r, 6 * r + 6))
     for a, b in ((0, 6 * r), (6 * r + 6, 24)):
         if a < b:
             copy("V", v("in2", a, b), v("pland", a, b))
-    copy("V", v("ysb", 0, C), v("ps", 2048, 2048 + C))
-    dma("Y", hbm(T.y[:, :]), v("ysb", 0, C), "dy")
     tr(v("plt", 0, 32), v("in2", 0, 32))
     for q in range(4):
         for e in range(2):

@@ -2,13 +2,13 @@ from concourse.bass import DstId, RemoteDMATransfer
 from concourse.mybir import dt, AluOpType as ALU, ActivationFunctionType as AF
 
 N, C, ROUNDS = 4, 384, 2
+M = N * C
 HC = C // 2
-SL = 400
-RW = 4 * SL
+TW = 7 * C
 BIG = 1e29
 F32, BF, I32, U16, CODE, U8 = "float32", "bfloat16", "int32", "uint16", "float8_e4m3fn_x4", "uint8"
 
-SCRATCH = {"ps": ("psum", [128, 4096], F32)}
+SCRATCH = {"ps": ("psum", [128, 4096], F32), "tab": ("sbuf", [128, 4, TW], BF)}
 
 
 def _sb(name, n, d):
@@ -20,7 +20,6 @@ for _t in range(3):
 for _t in range(ROUNDS):
     _sb("sh%d" % _t, 4 * C, BF); _sb("pq%d" % _t, C, CODE); _sb("pp%d" % _t, C, U8)
     _sb("lq%d" % _t, C, CODE); _sb("lp%d" % _t, C, U8)
-    _sb("tab%d" % _t, 4 * RW, BF)
     _sb("ug%d" % _t, 4 * C, BF); _sb("gq%d" % _t, C, CODE); _sb("gp%d" % _t, C, U8)
     _sb("oq%d" % _t, 128, CODE); _sb("op%d" % _t, 128, U8)
     _sb("mq%d" % _t, 352, CODE); _sb("mp%d" % _t, 352, U8)
@@ -30,20 +29,19 @@ for _n in ("u", "v"):
     _sb(_n + "t", 512, BF); _sb(_n + "q", 128, CODE); _sb(_n + "p", 128, U8)
 for _n, _w, _d in (
         ("wq", 512, CODE), ("wp", 512, U8), ("et", 2048, BF), ("eq", 512, CODE), ("ep", 512, U8),
-        ("aa", 1536, F32), ("sw", 1536, F32), ("call", 48, F32), ("g0", 768, F32), ("tt", 800, F32), ("lam", 1536, F32),
-        ("rr", 7 * RW, F32), ("gf", C, F32), ("tf", C, F32),
-        ("scraw", 56, I32), ("scl", 48, I32), ("lsc", 48, U16), ("ll0", 100, U16), ("ll1", 100, U16),
-        ("lf", 24, U16), ("ld", 96, U16),
-        ("wk", 320, F32), ("so", 136, F32), ("yy", 64, F32), ("fs", 64, F32),
-        ("idm", 128, F32), ("ic", 96, F32), ("i96", 96, F32), ("i12", 12, F32),
-        ("pint", 8, I32), ("col", 8, F32), ("bet", 96, F32),
+        ("ww", 2 * M, F32), ("aa", M, F32), ("g0", 768, F32), ("tt", 768, F32), ("gs", 6 * HC, F32), ("ts", HC, F32),
+        ("gf", C, F32), ("tf", C, F32), ("bet", 288, F32), ("beti", 48, I32),
+        ("scraw", 56, I32), ("sco", 12, I32), ("sci", 48, I32), ("scf", 72, F32), ("scl", 48, F32), ("lsc", 48, U16),
+        ("la", 12, U16), ("lf", 24, U16), ("ld", 24, U16),
+        ("wk", 320, F32), ("so", 208, F32), ("idm", 128, F32), ("i12", 12, F32),
+        ("pint", 8, I32), ("col", 8, F32), ("pw", 128, F32), ("pwi", 48, I32),
         ("ysb", C, F32), ("plsend", 24, F32), ("pland", 24, F32), ("in2", 32, F32), ("plt", 32, F32)):
     _sb(_n, _w, _d)
 
-SEMAPHORES = ["cV", "cS", "cT", "cG", "sent", "scarr", "plarr", "dx", "du", "dsc", "dsh", "dw", "dv", "dpad", "dy", "doc", "dpl"]
+SEMAPHORES = ["cV", "cS", "cT", "cG", "sent", "scarr", "plarr", "dx", "du", "dsc", "dsh0", "dsh1", "dw", "dv", "dpad", "dy", "doc", "dpl"]
 for _t in range(ROUNDS):
     SEMAPHORES += ["sarr%d" % _t, "p1arr%d" % _t, "dp1%d" % _t, "drep%d" % _t]
-    SEMAPHORES += ["p2arr%d_%d" % (_t, _k) for _k in range(N)]
+    SEMAPHORES += ["p2arr%d_%d" % (_t, _k) for _k in range(N)] + ["dpub%d_%d" % (_t, _k) for _k in range(6)]
 
 
 def _split(topo, cores, r):
@@ -71,12 +69,17 @@ def rank_program(g, core, T, topo):
     total = {}
     pool = []
 
-    def v(name, c0, c1, step=1, p0=0, p1=128):
-        ap = T[name][p0:p1, c0:c1:step] if step != 1 else T[name][p0:p1, c0:c1]
+    def v(name, c0, c1, step=1, p0=0, p1=128, ps=1):
+        rows = slice(p0, p1, ps) if ps != 1 else slice(p0, p1)
+        ap = T[name][rows, c0:c1:step] if step != 1 else T[name][rows, c0:c1]
         if name == "ps":
-            cols = frozenset(c // 512 for c in range(c0, c1, step))
-            return (ap, (name, 0, 128, cols))
+            return (ap, (name, 0, 128, frozenset(c // 512 for c in range(c0, c1, step))))
         return (ap, (name, p0, p1, frozenset(range(c0, c1, step))))
+
+    def tabv(b, c0, c1, p0=0, p1=128):
+        bs = range(4) if b is None else [b]
+        ap = T.tab[p0:p1, :, c0:c1] if b is None else T.tab[p0:p1, b, c0:c1]
+        return (ap, ("tab", p0, p1, frozenset(7 * x + s for x in bs for s in range(c0 // C, c1 // C))))
 
     def u8(x):
         return (x[0].bitcast(dt.uint8), x[1])
@@ -178,205 +181,231 @@ def rank_program(g, core, T, topo):
     def p2place(src, at):
         return (0, 128, 224)[[k for k in range(N) if k != at].index(src)]
 
-    def sgn(q, bit):
-        return -1 if q & bit else 1
+    SLOT, BACK = v("col", 2, 3), v("col", 3, 4)
 
-    def pads(t):
-        for s in range(4):
-            mset(v("tab%d" % t, 4 * SL * s, 4 * SL * s + 64), 0.0)
-
-    SH, PQ, P16, M1, M2 = [v("col", i, i + 1) for i in range(5)]
-
-    dma("Y", v("xt0", 0, 4 * C), hbm(T.x[:, :]), "dx")
-    dma("Y", v("ut", 0, 512), hbm(T.u[:, :]), "du")
     for q in range(4):
         for e in range(2):
             p = 32 * q + 16 * e
-            dma("S", v("scraw", 0, 54, 1, p, p + 16), hbm(T.sc[:, 24 * e + 6 * q:24 * e + 6 * q + 54]), "dsc")
+            dma("SY"[e], v("scraw", 0, 54, 1, p, p + 16), hbm(T.sc[:, 24 * e + 6 * q:24 * e + 6 * q + 54]), "dsc")
+    dma("Y", v("xt0", 0, 4 * C), hbm(T.x[:, :]), "dx")
+    dma("S", v("ut", 0, 512), hbm(T.u[:, :]), "du")
     for k in range(4):
         for q in range(4):
             dma("Y", v("sh0", 384 * k, 384 * k + 384, 1, 32 * q, 32 * q + 32),
-                hbm(T.x[32 * k:32 * k + 32, 384 * q:384 * q + 384]), "dsh")
-    iota(v("ic", 0, 96), [[1, 96]], 0, 0)
+                hbm(T.x[32 * k:32 * k + 32, 384 * q:384 * q + 384]), "dsh0")
     iota(v("pint", 0, 1), [[0, 1]], 0, 1, False)
     iota(v("idm", 0, 128), [[-1, 128]], 0, 1)
+    iota(v("bet", 48, 96), [[0, 16], [4, 3]], 0, 0)
+    iota(v("bet", 96, 144), [[0, 4], [96, 4], [0, 3]], 0, 1)
+    iota(v("i12", 0, 12), [[32, 6], [192, 2]], 0, 1)
     for q in range(4):
-        iota(v("bet", 0, 16, 1, 32 * q, 32 * q + 32), [[96, 4], [sgn(q, 2) * 2 * SL, 2], [sgn(q, 1) * SL, 2]], 16 + SL * q, 0)
+        iota(v("bet", 0, 48, 1, 32 * q, 32 * q + 32), [[1 - 2 * (q % 2), 2], [2 - 4 * (q // 2), 2], [0, 12]], q, 0)
     mset(v("et", 0, 2048), 0.0)
-    mset(v("so", 0, 136), 0.0)
-    mset(v("wk", 0, 1), -BIG)
-    mset(v("wk", 67, 112, 4), -BIG)
-    for i in range(3):
-        mset(v("wk", 64 + i, 112, 4), BIG)
-    for i in range(16):
-        copy("S", v("aa", 96 * i, 96 * i + 96), v("ic", 0, 96))
-    for i, m in enumerate((16, 96, 112, 15)):
+    for i, m in enumerate((96, 112, 32, 64)):
         ts(v("pint", 1 + i, 2 + i), v("pint", 0, 1), m, ALU.bitwise_and)
+    mset(v("aa", 0, 2 * C), 0.0)
+    copy("V", v("col", 4, 8), v("pint", 1, 5))
     ts(v("et", 0, 512, 4), v("idm", 0, 128), 0.0, ALU.is_equal)
     for b in range(1, 4):
         copy("S", v("et", 512 * b + b, 512 * b + 512, 4), v("et", 0, 512, 4))
+    copy("S", v("aa", 2 * C, M), v("aa", 0, 2 * C))
+    for h in range(2):
+        copy("S", v("ww", 2 * C * h, 2 * C * h + 2 * C), v("aa", 0, 2 * C))
     for kk in range(2):
         for h in range(2):
-            copy("V", v("scl", 12 * r + 2 * kk + h, 12 * r + 12, 4), v("scraw", 48 * kk + h, 48 * kk + 6, 2))
+            copy("V", v("sco", 2 * kk + h, 12, 4), v("scraw", 48 * kk + h, 48 * kk + 6, 2))
+    mset(v("so", 0, 208), 0.0)
+    for i, m in enumerate((32, 64, 31)):
+        ts(v("sci", 12 * i, 12 * i + 12), v("sco", 0, 12), m, ALU.bitwise_and)
+    ts(v("sci", 36, 48), v("sco", 0, 12), 7, ALU.logical_shift_right)
+    ts(v("scf", 0, 12), v("sci", 0, 12), v("col", 6, 7), ALU.not_equal, 768.0, ALU.mult)
+    ts(v("scf", 12, 24), v("sci", 12, 24), v("col", 7, 8), ALU.not_equal, 384.0, ALU.mult)
+    ts(v("scf", 24, 36), v("sci", 36, 48), 32.0, ALU.mult)
+    mset(v("wk", 0, 1), -BIG)
+    mset(v("wk", 67, 112, 4), -BIG)
+    tt_(v("scf", 48, 60), v("scf", 0, 12), v("scf", 12, 24), ALU.add)
+    tt_(v("scf", 60, 72), v("scf", 24, 36), v("sci", 24, 36), ALU.add)
+    quant("xq0", "xs0", "xt0", C)
+    tt_(v("scl", 12 * r, 12 * r + 12), v("scf", 48, 60), v("scf", 60, 72), ALU.add)
     send_all(v("scl", 12 * r, 12 * r + 12), v("scl", 12 * r, 12 * r + 12), "scarr")
     arrive("scarr", sum(n_all(k) for k in others), [v("scl", 12 * k, 12 * k + 12) for k in others])
-    iota(v("bet", 16, 32), [[96, 16]], 0, 0)
-    iota(v("i96", 0, 96), [[32, 48], [0, 2]], 0, 1)
-    iota(v("i12", 0, 12), [[32, 12]], 16, 1)
+    quant("uq", "up", "ut", 128)
+    tt_(v("bet", 144, 192), v("bet", 0, 48), v("bet", 48, 96), ALU.add)
+    for i in range(3):
+        mset(v("wk", 64 + i, 112, 4), BIG)
+    ts(v("bet", 192, 240), v("bet", 144, 192), 1.0 / 3, ALU.mult, 0.5 / 3 - 0.5, ALU.add)
+    ts(v("bet", 0, 48), v("bet", 144, 192), 32.0, ALU.mult, v("col", 4, 5), ALU.subtract)
+
+    def late_setup():
+        copy("V", v("beti", 0, 48), v("bet", 192, 240))
+        tt_(v("bet", 48, 96), v("bet", 0, 48), v("bet", 96, 144), ALU.add)
+        ts(SLOT, v("pint", 1, 2), -12.0, ALU.mult, 3.0 * C, ALU.add)
+        ts(BACK, v("pint", 1, 2), 12.0, ALU.mult, -3.0 * C, ALU.add)
+        ts(v("bet", 240, 288), v("beti", 0, 48), 288.0, ALU.mult)
+        quant("pq0", "pp0", "sh0", C)
+        for e in range(2):
+            tt_(v("aa", 16 * e + 1, M, 32), v("bet", 48, 96), v("bet", 240, 288), ALU.add)
+        ts(v("col", 0, 1), v("pint", 1, 2), 11.0, ALU.mult)
+        quant("eq", "ep", "et", 512)
+        if r == 0:
+            ts(v("lf", 0, 24, 2), v("i12", 0, 12), v("col", 0, 1), ALU.add)
 
     def late_loads():
         dma("Y", u8(v("wq", 0, 512)), hbm(T.wc[:, :]), "dw")
         dma("Y", v("wp", 0, 512), hbm(T.ws[:, :]), "dw")
-        dma("Y", v("vt", 0, 512), hbm(T.v[:, :]), "dv")
         for t in range(ROUNDS):
             for c0 in (96, 320):
                 dma("Y", u8(v("mq%d" % t, c0, c0 + 32)), u8(v("xq0", 0, 32)), "dpad")
                 dma("Y", v("mp%d" % t, c0, c0 + 32), v("xs0", 0, 32), "dpad")
+        dma("Y", v("vt", 0, 512), hbm(T.v[:, :]), "dv")
 
-    def late_setup():
-        copy("V", v("col", 0, 3), v("pint", 1, 4))
-        ts(M1, v("pint", 4, 5), 1.0, ALU.is_equal)
-        ts(M2, v("pint", 4, 5), 2.0, ALU.is_equal)
-        copy("V", v("bet", 32, 48, 1, 0, 64), v("bet", 0, 16, 1, 64, 128))
-        copy("V", v("bet", 32, 48, 1, 64, 128), v("bet", 0, 16, 1, 0, 64))
-        tt_(v("bet", 48, 64), v("bet", 16, 32), v("bet", 0, 16), ALU.subtract)
-        ts(v("aa", 1, 1536, 16), v("i96", 0, 96), PQ, ALU.subtract)
-        tt_(v("bet", 64, 80), v("bet", 32, 48), v("bet", 0, 16), ALU.subtract)
-        ts(v("bet", 16, 32), v("bet", 48, 64), M2, ALU.mult)
-        ts(v("lf", 0, 24, 2), v("i12", 0, 12), P16, ALU.subtract)
-        ts(v("bet", 32, 48), v("bet", 64, 80), M1, ALU.mult)
-        tt_(v("bet", 48, 64), v("bet", 16, 32), v("bet", 0, 16), ALU.add)
-        quant("eq", "ep", "et", 512)
-        tt_(v("bet", 80, 96), v("bet", 48, 64), v("bet", 32, 48), ALU.add)
+    def lay_table(s):
+        def shift(ds):
+            def f():
+                for d in ds:
+                    a, b = max(0, -32 * d), min(128, 128 - 32 * d)
+                    dma("Y", tabv(None, C * (3 + d), C * (4 + d), a, b), tabv(None, 3 * C, 4 * C, a + 32 * d, b + 32 * d), "drep" + s)
+            return f
+        return [shift((1, -1)), shift((2, 3)), shift((-2, -3))]
 
-    def places():
-        for i in range(16):
-            o, a, bi = v("lam", 96 * i, 96 * i + 96), v("ic", 0, 96), v("bet", 80 + i, 81 + i)
-            add("S", lambda q, o=o, a=a, bi=bi: q.activation(o[0], a[0], AF.Identity, bias=bi[0]), [o], [a, bi])
-
-    def score_rows(src, m0, m1, s0, engs):
+    def spread(src, runs, s0, e1, e2):
+        for m0, m1 in runs:
+            for e in range(2):
+                copy(e1[e], v("aa", 32 * m0 + 16 * e, 32 * m1, 32), v(src, m0 - s0, m1 - s0))
+                for a, b in ((0, 64), (64, 0)):
+                    copy(e1[e], v("aa", C + 32 * m0 + 16 * e, C + 32 * m1, 32, a, a + 64), v(src, m0 - s0, m1 - s0, 1, b, b + 64))
         for q in range(4):
-            for a in range(4):
-                copy(engs[a % 2], v("call", 4 * m0 + a, 4 * m1, 4, 32 * q, 32 * q + 32), v(src, s0, s0 + m1 - m0, 1, 32 * a, 32 * a + 32))
-        copy(engs[0], v("aa", 128 * m0, 128 * m1, 32), v("call", 4 * m0, 4 * m1))
-        copy(engs[1], v("aa", 128 * m0 + 16, 128 * m1, 32), v("call", 4 * m0, 4 * m1))
-        return v("sw", 128 * m0, 128 * m1), v("aa", 128 * m0, 128 * m1)
+            o = 32 * (q ^ 1)
+            copy(e2, v("aa", 2 * C, 4 * C, 16, 32 * q, 32 * q + 32), v("aa", 0, 2 * C, 16, o, o + 32))
 
-    def step(gi, win, lst, last):
-        if last:
-            cuts = (("V", 0, 24), ("S", 40, 100), ("V", 24, 40))
-        elif gi == 0:
-            cuts = (("S", 20, 50), ("V", 0, 20), ("S", 50, 100))
-        else:
-            cuts = (("S", 24, 50), ("V", 0, 24), ("S", 50, 100))
-        for eng, a, b in cuts:
-            gather(eng, v("rr", RW * gi + 16 * a, RW * gi + 16 * b), win, v(lst, a, b))
+    def rows(runs):
+        for x in range(4):
+            for m0, m1 in runs:
+                tr(v("ww", M + C * x + 32 * m0, M + C * x + 32 * m1), v("aa", C * x + 32 * m0, C * x + 32 * m1))
 
-    def wrap(gi, lst):
-        tr(v("tt", 0, 800), v("rr", RW * gi, RW * gi + 800))
-        ts(v(lst, 0, 50), v("tt", 0, 800, 16), SH, ALU.subtract)
-        for a, b in ((0, 64), (64, 0)):
-            ts(v(lst, 50, 100, 1, a, a + 64), v("tt", 1, 800, 16, b, b + 64), v("col", 0, 1, 1, b, b + 64), ALU.subtract)
+    def publish(j, s, qs):
+        for x in range(8):
+            dma(qs[x % len(qs)], v("ww", M * (j % 2), M * (j % 2) + M, 1, 16 * x, 16 * x + 1),
+                v("gs", HC * j, HC * j + HC, 1, 0, 128, 16), "dpub%s_%d" % (s, j))
 
-    def row(gi):
-        return v("rr", RW * gi, RW * gi + RW)
-
-    quant("xq0", "xs0", "xt0", C)
-    quant("uq", "up", "ut", 128)
     for t in range(ROUNDS):
         s = str(t)
         X, XQ, XS = "xt" + s, "xq" + s, "xs" + s
-        shuffle = [(q, k) for k in range(4) for q in range(4)] if t else []
-        for q, k in shuffle[:5]:
-            copy("S", v("sh" + s, 384 * k, 384 * k + 384, 1, 32 * q, 32 * q + 32), v(X, 384 * q, 384 * q + 384, 1, 32 * k, 32 * k + 32))
-        for i in range(3):
+        shuffle = [(q, k) for k in range(4) for q in (2, 3)] if t else []
+
+        def shuf(e, part):
+            for q, k in part:
+                copy(e, v("sh" + s, 384 * k, 384 * k + 384, 1, 32 * q, 32 * q + 32), v(X, 384 * q, 384 * q + 384, 1, 32 * k, 32 * k + 32))
+        shuf("S", shuffle[:3])
+        shuf("V", shuffle[3:5])
+        for i in range(1 if t else 0, 3):
             mm(i, XQ, XS, 128 * i, "uq", "up", 0, 128)
         copy("V", v("ssend" + s, 0, 3), v("ps", 0, 1536, 512))
         send_all(v("ssend" + s, 0, 3), v("sland" + s, 3 * r, 3 * r + 3), "sarr" + s)
         arrive("sarr" + s, sum(n_all(k) for k in others), [v("sland" + s, 3 * k, 3 * k + 3) for k in others])
-        for q, k in shuffle[5:]:
-            copy("V", v("sh" + s, 384 * k, 384 * k + 384, 1, 32 * q, 32 * q + 32), v(X, 384 * q, 384 * q + 384, 1, 32 * k, 32 * k + 32))
+        shuf("V", shuffle[5:])
         if t == 0:
             late_setup()
-        own = score_rows("ssend" + s, 3 * r, 3 * r + 3, 0, "SS")
-        quant("pq" + s, "pp" + s, "sh" + s, C)
+        else:
+            quant("pq" + s, "pp" + s, "sh" + s, C)
         send_tiles("pq" + s, "pp" + s, "lq" + s, "lp" + s, lambda k: 96 * r, "p1arr" + s)
         dma("Y", u8(v("lq" + s, 96 * r, 96 * r + 96)), u8(v("pq" + s, 96 * r, 96 * r + 96)), "dp1" + s)
         dma("Y", v("lp" + s, 96 * r, 96 * r + 96), v("pp" + s, 96 * r, 96 * r + 96), "dp1" + s)
         arrive("p1arr" + s, sum(n_tiles(k) for k in others),
                [v(n + s, 96 * k, 96 * k + 96) for k in others for n in ("lq", "lp")])
-        pads(t)
-        tr(*own)
+        spread("ssend" + s, [(3 * r, 3 * r + 3)], 3 * r, "SS", "S")
+        rows([(3 * r, 3 * r + 3)])
         if t == 0:
-            copy("V", v("lsc", 0, 48), v("scl", 0, 48))
-        for m0, m1 in ((0, 3 * r), (3 * r + 3, 12)):
-            if m0 < m1:
-                tr(*score_rows("sland" + s, m0, m1, m0, "VS"))
-        if t == 0:
-            places()
-        gather("V", v("g0", 0, 384), v("sw", 0, 1536), v("lsc", 0, 24))
-        gather("S", v("g0", 384, 768), v("sw", 0, 1536), v("lsc", 24, 48))
-        tr(v("tt", 0, 768), v("g0", 0, 768))
-        TAB = "tab" + s
-        for b in range(4):
-            mm(4 + b, "eq", "ep", 128 * b, "lq" + s, "lp" + s, 0, C)
-        for b in range(4):
-            copy("S", v(TAB, 64 + b, 64 + 4 * C, 4), v("ps", 512 * (4 + b), 512 * (4 + b) + C))
-        for a, b in ((0, 64), (64, 0)):
-            dma("Y", v(TAB, 8 * SL + 64, 12 * SL, 1, a, a + 64), v(TAB, 64, 4 * SL, 1, b, b + 64), "drep" + s)
-        for x in (1, 3):
-            for q in range(4):
-                dma("Y", v(TAB, 4 * SL * x + 64, 4 * SL * (x + 1), 1, 32 * q, 32 * q + 32),
-                    v(TAB, 64, 4 * SL, 1, 32 * (q ^ x), 32 * (q ^ x) + 32), "drep" + s)
-        if t == 0:
-            late_loads()
+            for h in range(2):
+                for x in range(4):
+                    copy("V", v("lsc", 4 * h + x, 48, 8), v("scl", 24 * h + x, 24 + 24 * h, 4))
+        far = [x for x in ((0, 3 * r), (3 * r + 3, 12)) if x[0] < x[1]]
+        spread("sland" + s, far, 0, "VS", "S")
+        rows(far)
+        cuts = (("V", 0, 10), ("S", 20, 32), ("V", 10, 20), ("S", 32, 48))
+        for e, a, b in cuts:
+            gather(e, v("g0", 16 * a, 16 * b), v("ww", M, 2 * M), v("lsc", a, b))
+        for e, a, b in cuts:
+            tr(v("tt", 16 * a, 16 * b), v("g0", 16 * a, 16 * b))
         SC, NB = v("tt", 0, 768, 16), v("tt", 1, 768, 16)
         scan(v("wk", 1, 49), SC, v("wk", 64, 112), -BIG, ALU.max, ALU.min)
         tt_(v("wk", 192, 240), SC, v("wk", 0, 48), ALU.is_gt)
         tt_(v("wk", 128, 176), SC, v("wk", 0, 48), ALU.is_le)
         tt_(v("wk", 256, 304), v("wk", 192, 240), NB, ALU.mult)
-        scan(v("so", 4, 52), v("wk", 128, 176), v("wk", 256, 304), 0.0, ALU.mult, ALU.add)
-        tr(v("yy", 0, 32), v("so", 3, 131, 4))
-        tr(v("yy", 32, 64), v("so", 7, 135, 4))
-        copy("V", v("fs", 1, 25, 2), v("so", 7, 52, 4))
-        tr(v("fs", 0, 64, 2), v("yy", 16, 48))
-        for x in (1, 0, 2, 3):
-            n = (128, 32, 64, 32)[x]
-            for p in range(0, 128, n):
-                o = p ^ (32 * x)
-                copy("V", v("ll0", 25 * x, 25 * x + 25, 1, p, p + n), v("fs", 0, 25, 1, o, o + n))
-        g0 = 2 * r
-        step(0, v("lam", 0, 1536), "ll0", g0 == 0)
-        for gi in range(g0):
-            lst = "ll%d" % ((gi + 1) % 2)
-            wrap(gi, lst)
-            step(gi + 1, row(gi), lst, gi + 1 == g0)
-        tr(v("tt", 0, 384), v("rr", RW * g0, RW * g0 + 384))
-        ts(v("lf", 1, 24, 2), v("tt", 16, 384, 32), SH, ALU.subtract)
-        gather("V", v("gf", 0, 192), row(g0), v("lf", 0, 12))
-        gather("S", v("gf", 192, 384), row(g0), v("lf", 12, 24))
-        tr(v("tf", 0, 384), v("gf", 0, 384))
-        for b in (2, 0, 3, 1):
-            ts(v("ld", 24 * b, 24 * b + 24), v("tf", 0, 384, 16), 4.0, ALU.mult, float(b), ALU.add)
+        scan(v("so", 0, HC, 4), v("wk", 128, 176), v("wk", 256, 304), 0.0, ALU.mult, ALU.add)
+        tr(v("gs", 0, HC), v("so", 12, 12 + HC))
+        publish(0, s, "YS")
+        copy("V", v("lf", 1, 24, 2) if r == 0 else v("la", 0, 12), v("so", 12, 12 + HC, 16))
+        if t == 0:
+            mset(v("in2", 0, 32), 0.0)
+        for b in range(4):
+            mm(4 + b, "eq", "ep", 128 * b, "lq" + s, "lp" + s, 0, C)
+        for b in range(4):
+            copy("VSVS"[b], tabv(b, 3 * C, 4 * C), v("ps", 512 * (4 + b), 512 * (4 + b) + C))
+        lay = lay_table(s)
+        late = [late_loads] if t == 0 else []
+        after = ({0: lay + late}, {0: lay[:1], 2: lay[1:] + late}, {0: lay[:1], 2: lay[1:2], 4: lay[2:], 6: late},
+                 {0: lay[:1], 2: lay[1:2], 4: lay[2:], 10: late})[r]
+        for f in after[0]:
+            f()
+        for st in range(1, 4 * r + 1):
+            w = max(0, (st - 3) // 2) % 2
+            j = st // 2
+            pub = st % 2 == 0 and j < 2 * r
+            src = HC * j if pub else 0
+            for h in range(3):
+                gather("S", v("gs", src + 64 * h, src + 64 * h + 64), v("ww", M * w, M * w + M), v("la", 4 * h, 4 * h + 4))
+            if pub:
+                publish(j, s, "Y")
+            for h in range(4):
+                if h < 3:
+                    tr(v("ts", 64 * h, 64 * h + 64), v("gs", src + 64 * h, src + 64 * h + 64))
+                if h > 0:
+                    a = v("ts", 64 * h - 64, 64 * h, 16)
+                    if st == 4 * r:
+                        ts(v("lf", 8 * h - 7, 8 * h, 2), a, float(M), ALU.add)
+                    else:
+                        copy("V", v("la", 4 * h - 4, 4 * h), a)
+                    if st == 4 * r - 2:
+                        copy("V", v("lf", 8 * h - 8, 8 * h, 2), a)
+            for f in after.get(st, []):
+                f()
+        for h in range(3):
+            gather("SSV"[h], v("gf", 128 * h, 128 * h + 128), v("ww", 0, 2 * M), v("lf", 8 * h, 8 * h + 8))
+        for h in range(3):
+            tr(v("tf", 128 * h, 128 * h + 128), v("gf", 128 * h, 128 * h + 128))
+        for x in range(4):
+            ts(v("ld", 12 * (x // 2) + x % 2, 12 * (x // 2) + 12, 2), v("tf", 16 * x, C, 64), SLOT, ALU.add)
         n1 = 18 if r == N - 1 else 24
-        for b in (2, 0, 3, 1):
-            gather("VVSS"[b], v("ug" + s, b, 64 * n1, 4), v(TAB, 0, 4 * RW), v("ld", 24 * b, 24 * b + n1))
+
+        def pick(a, b):
+            for x in (2, 0, 3, 1):
+                gather("VVSS"[x], v("ug" + s, 64 * a + x, 64 * b, 4), tabv(x, 0, TW), v("ld", a, b))
+        pick(0, n1)
         quant("gq" + s, "gp" + s, "ug" + s, 16 * n1)
         send_tiles("gq" + s, "gp" + s, "mq" + s, "mp" + s, lambda k: p2place(r, k), "p2arr%d_%d" % (t, r))
         for k in others:
             c0 = p2place(k, r)
             arrive("p2arr%d_%d" % (t, k), n_tiles(k), [v(n + s, c0, c0 + 96) for n in ("mq", "mp")])
         if n1 < 24:
-            for b in (2, 3, 0, 1):
-                gather("VSSS"[b], v("ug" + s, 64 * n1 + b, 4 * C, 4), v(TAB, 0, 4 * RW), v("ld", 24 * b + n1, 24 * b + 24))
+            pick(n1, 24)
             quant("oq" + s, "op" + s, "ug" + s, 128, C - 128)
+        fill = []
         if t == 0:
             quant("vq", "vp", "vt", 128)
-            mset(v("in2", 0, 32), 0.0)
         else:
-            copy("S", v("plsend", 0, 24), v("tf", 2, 384, 16))
-            send_each([v("plsend", 6 * k, 6 * k + 6) for k in others], [v("pland", 6 * r, 6 * r + 6) for k in others], 2, "plarr")
-            arrive("plarr", sum(n_each(k, 2) for k in others), [v("pland", 6 * k, 6 * k + 6) for k in others])
+            def pl_send():
+                tt_(v("plsend", 0, 24), v("pw", 96, 120), v("pw", 56, 80), ALU.add)
+                send_each([v("plsend", 6 * k, 6 * k + 6) for k in others], [v("pland", 6 * r, 6 * r + 6) for k in others], 2, "plarr")
+                arrive("plarr", sum(n_each(k, 2) for k in others), [v("pland", 6 * k, 6 * k + 6) for k in others])
+            ts(v("pw", 0, 24), v("ld", 0, 24), BACK, ALU.add)
+            fill = [lambda: (ts(v("pw", 32, 56), v("pw", 0, 24), 1.0 / 96, ALU.mult, 0.5 / 96 - 0.5, ALU.add),
+                             ts(v("pw", 56, 80), v("pw", 0, 24), 1.0 / C, ALU.mult, 0.5 / C - 0.5, ALU.add)),
+                    lambda: copy("V", v("pwi", 0, 48), v("pw", 32, 80)),
+                    lambda: (ts(v("pw", 32, 56), v("pwi", 0, 24), 288.0, ALU.mult),
+                             ts(v("pw", 56, 80), v("pwi", 24, 48), -1440.0, ALU.mult)),
+                    lambda: tt_(v("pw", 96, 120), v("pw", 32, 56), v("pw", 0, 24), ALU.add),
+                    pl_send]
         H, HQ, HP = "ht" + s, "hq" + s, "hp" + s
         XN, XQN, XSN = "xt%d" % (t + 1), "xq%d" % (t + 1), "xs%d" % (t + 1)
         for i, k in enumerate([r] + others if n1 == 24 else others + [r]):
@@ -394,7 +423,10 @@ def rank_program(g, core, T, topo):
                 for b in (0, 2, 1, 3):
                     for q in (2 * h, 2 * h + 1):
                         c = 512 * (base + b) + c0 - lo
-                        copy("VVSS"[b], v(H, 384 * q + b, 384 * q + 384, 4, 32 * k, 32 * k + 32), v("ps", c, c + 96, 1, 32 * q, 32 * q + 32))
+                        copy("VVSV"[b] if (h == 1 and i < N - 1) else "VVSS"[b],
+                             v(H, 384 * q + b, 384 * q + 384, 4, 32 * k, 32 * k + 32), v("ps", c, c + 96, 1, 32 * q, 32 * q + 32))
+                if fill:
+                    fill.pop(0)()
                 if i == N - 1:
                     quant(HQ, HP, H, HC, HC * h, HC * h)
                     for b in (0, 2, 1, 3):
@@ -407,23 +439,33 @@ def rank_program(g, core, T, topo):
                 else:
                     add("S", lambda q, o=o, a=a: q.activation(o[0], a[0], AF.Relu, scale=0.03125), [o], [a])
             quant(XQN, XSN, XN, HC, HC * h, HC * h)
+            if t < ROUNDS - 1 and h == 0:
+                mm(0, XQN, XSN, 0, "uq", "up", 0, 128)
+                for k in range(4):
+                    for q in range(2):
+                        dma("Y", v("sh1", 384 * k, 384 * k + 384, 1, 32 * q, 32 * q + 32),
+                            v(XN, 384 * q, 384 * q + 384, 1, 32 * k, 32 * k + 32), "dsh1")
+            if t == ROUNDS - 1:
+                if h == 0:
+                    copy("V", v("in2", 6 * r, 6 * r + 6), v("plsend", 6 * r, 6 * r + 6))
+                dma("Y", hbm(T.oc[:, 4 * HC * h:4 * HC * (h + 1)]), u8(v("xq2", HC * h, HC * h + HC)), "doc")
 
     for h in range(2):
         mm(h, "vq", "vp", 0, "xq2", "xs2", HC * h, HC)
-    copy("S", v("ysb", 0, HC), v("ps", 0, HC))
-    dma("Y", hbm(T.oc[:, :]), u8(v("xq2", 0, C)), "doc")
-    copy("V", v("ysb", HC, C), v("ps", 512, 512 + HC))
-    dma("Y", hbm(T.y[:, :]), v("ysb", 0, C), "dy")
-    for k in range(4):
-        dma("S", hbm(T.osc[4 * k:4 * k + 4, :]), v("xs2", 0, C, 1, 32 * k, 32 * k + 4), "doc")
-    copy("V", v("in2", 6 * r, 6 * r + 6), v("plsend", 6 * r, 6 * r + 6))
     for a, b in ((0, 6 * r), (6 * r + 6, 24)):
         if a < b:
             copy("V", v("in2", a, b), v("pland", a, b))
+    copy("S", v("ysb", 0, HC), v("ps", 0, HC))
     tr(v("plt", 0, 32), v("in2", 0, 32))
+    dma("S", hbm(T.y[:, 0:HC]), v("ysb", 0, HC), "dy")
+    copy("V", v("ysb", HC, C), v("ps", 512, 512 + HC))
+    for k in range(4):
+        dma("SY"[k % 2], hbm(T.osc[4 * k:4 * k + 4, :]), v("xs2", 0, C, 1, 32 * k, 32 * k + 4), "doc")
     for q in range(4):
-        for e in range(2):
-            dma("YS"[e], hbm(T.pl[e:8:2, 96 * q:96 * q + 96]), v("plt", 16 * e, 16 * e + 16, 1, 32 * q, 32 * q + 24), "dpl")
+        dma("S", hbm(T.pl[0:8:2, 96 * q:96 * q + 96]), v("plt", 0, 16, 1, 32 * q, 32 * q + 24), "dpl")
+        if q == 1:
+            dma("Y", hbm(T.y[:, HC:C]), v("ysb", HC, C), "dy")
+        dma("Y", hbm(T.pl[1:8:2, 96 * q:96 * q + 96]), v("plt", 16, 32, 1, 32 * q, 32 * q + 24), "dpl")
 
     def meet(a, b):
         return a[0] == b[0] and a[1] < b[2] and b[1] < a[2] and not a[3].isdisjoint(b[3])
@@ -478,7 +520,6 @@ def rank_program(g, core, T, topo):
                 ins.then_inc(T.sem["c" + op["e"]], 1)
         elif op["sem"] != "sent":
             ins.then_inc(T.sem[op["sem"]], 16)
-    for e, n in sorted(count.items()):
-        g.wait_ge(T.sem["c" + e], n)
     for name in sorted(total):
-        g.wait_ge(T.sem[name], total[name])
+        if max([n for (e, x), n in waited.items() if x == name] + [0]) < total[name]:
+            g.wait_ge(T.sem[name], total[name])

@@ -11,36 +11,28 @@ F32, BF, I32, U16, CODE, U8 = "float32", "bfloat16", "int32", "uint16", "float8_
 SCRATCH = {"ps": ("psum", [128, 4096], F32), "tab": ("sbuf", [128, 4, TW], BF)}
 
 
-def _sb(name, n, d):
-    SCRATCH[name] = ("sbuf", [128, n], d)
+def _sb(d, **names):
+    for name, n in names.items():
+        SCRATCH[name] = ("sbuf", [128, n], d)
 
 
-for _t in range(3):
-    _sb("xt%d" % _t, 4 * C, BF); _sb("xq%d" % _t, C, CODE); _sb("xs%d" % _t, C, U8)
 for _t in range(ROUNDS):
-    _sb("sh%d" % _t, 4 * C, BF); _sb("pq%d" % _t, C, CODE); _sb("pp%d" % _t, C, U8)
-    _sb("lq%d" % _t, C, CODE); _sb("lp%d" % _t, C, U8)
-    _sb("ug%d" % _t, 4 * C, BF); _sb("gq%d" % _t, C, CODE); _sb("gp%d" % _t, C, U8)
-    _sb("oq%d" % _t, 128, CODE); _sb("op%d" % _t, 128, U8)
-    _sb("mq%d" % _t, 352, CODE); _sb("mp%d" % _t, 352, U8)
-    _sb("ht%d" % _t, 4 * C, BF); _sb("hq%d" % _t, C, CODE); _sb("hp%d" % _t, C, U8)
-    _sb("ssend%d" % _t, 4, F32); _sb("sland%d" % _t, 12, F32)
-for _n in ("u", "v"):
-    _sb(_n + "t", 512, BF); _sb(_n + "q", 128, CODE); _sb(_n + "p", 128, U8)
-for _n, _w, _d in (
-        ("wq", 512, CODE), ("wp", 512, U8), ("et", 2048, BF), ("eq", 512, CODE), ("ep", 512, U8),
-        ("ww", 2 * M, F32), ("aa", M, F32), ("g0", 768, F32), ("tt", 768, F32), ("gs", 6 * HC, F32), ("ts", HC, F32),
-        ("gf", C, F32), ("tf", C, F32), ("bet", 288, F32), ("beti", 48, I32),
-        ("scraw", 56, I32), ("sco", 12, I32), ("sci", 48, I32), ("scf", 72, F32), ("scl", 48, F32), ("lsc", 48, U16),
-        ("la", 12, U16), ("lf", 24, U16), ("ld", 24, U16),
-        ("wk", 320, F32), ("so", 208, F32), ("idm", 128, F32), ("i12", 12, F32),
-        ("pint", 8, I32), ("col", 8, F32), ("pw", 128, F32), ("pwi", 48, I32),
-        ("ysb", C, F32), ("plsend", 24, F32), ("pland", 24, F32), ("in2", 32, F32), ("plt", 32, F32)):
-    _sb(_n, _w, _d)
+    for _n, _w in (("p", C), ("l", C), ("g", C), ("b", C), ("o", 128), ("m", 352), ("h", C)):
+        _sb(CODE, **{"%sq%d" % (_n, _t): _w}); _sb(U8, **{"%sp%d" % (_n, _t): _w})
+    _sb(BF, **{"sh%d" % _t: M, "ug%d" % _t: M, "ht%d" % _t: M, "hs%d" % _t: 2 * C})
+    _sb(F32, **{"ssend%d" % _t: 4, "sland%d" % _t: 12})
+_sb(BF, xt0=M, xt1=M, xt2=M, ut=512, vt=512, et=2048)
+_sb(CODE, xq0=C, xq1=C, xq2=C, uq=128, vq=128, wq=512, eq=512)
+_sb(U8, xs0=C, xs1=C, xs2=C, up=128, vp=128, wp=512, ep=512)
+_sb(F32, ww=2 * M, aa=M, g0=768, tt=768, gs=6 * HC, ts=HC, gf=C, tf=C, bet=288, scf=280, scl=48, wk=320, so=224, idm=128,
+    i12=12, col=8, pw=128, ysb=C, plsend=24, pland=24, in2=32, plt=32)
+_sb(I32, beti=48, scraw=56, sci=224, pint=8, pwi=48)
+_sb(U16, lsc=48, la=12, lf=24, ld=24)
 
-SEMAPHORES = ["cV", "cS", "cT", "cG", "sent", "scarr", "plarr", "dx", "du", "dsc", "dsh0", "dsh1", "dw", "dv", "dpad", "dy", "doc", "dpl"]
+SEMAPHORES = ["cV", "cS", "cT", "cG", "sent", "scarr", "plarr", "dx0", "dx1", "dx2", "du", "dsc", "dsh0", "dsh1",
+              "dw", "dv", "dpad", "dy", "doc", "dpl"]
 for _t in range(ROUNDS):
-    SEMAPHORES += ["sarr%d" % _t, "p1arr%d" % _t, "dp1%d" % _t, "drep%d" % _t]
+    SEMAPHORES += ["sarr%d" % _t, "p1arr%d" % _t, "dp1%d" % _t, "drep%d" % _t, "dh%d" % _t]
     SEMAPHORES += ["p2arr%d_%d" % (_t, _k) for _k in range(N)] + ["dpub%d_%d" % (_t, _k) for _k in range(6)]
 
 
@@ -52,10 +44,7 @@ def _split(topo, cores, r):
 
 
 def _mask(es):
-    m = 0
-    for e in es:
-        m |= 1 << e
-    return m
+    return sum(1 << e for e in es)
 
 
 def rank_program(g, core, T, topo):
@@ -64,10 +53,11 @@ def rank_program(g, core, T, topo):
         return
     cores = T.cores
     others = [k for k in range(N) if k != r]
+    last = r == N - 1
+    near = ([k for k in range(N - 1) if topo.same_plane(topo.chip(cores[k]), topo.chip(cores[-1]))] + [N - 2])[0]
+    order = [k for k in range(N - 1) if k != near] + [near, N - 1] if last else list(range(N))
     queue = {"V": g.vector, "S": g.scalar, "T": g.tensor, "G": g, "Y": g.sync}
-    ops = []
-    total = {}
-    pool = []
+    ops, total, pool = [], {}, []
 
     def v(name, c0, c1, step=1, p0=0, p1=128, ps=1):
         rows = slice(p0, p1, ps) if ps != 1 else slice(p0, p1)
@@ -98,17 +88,13 @@ def rank_program(g, core, T, topo):
     def hbm(ap):
         return (ap, None)
 
-    def copy(eng, out, in_):
+    def copy(eng, out, in_, off=None):
+        src = in_[0] if off is None else in_[0].indirect(off[0])
+        ins = [in_] if off is None else [in_, off]
         if eng == "V":
-            add("V", lambda q: q.tensor_copy(out[0], in_[0]), [out], [in_])
+            add("V", lambda q: q.tensor_copy(out[0], src), [out], ins)
         else:
-            add("S", lambda q: q.activation(out[0], in_[0], AF.Copy), [out], [in_])
-
-    def gather(eng, out, win, off):
-        if eng == "V":
-            add("V", lambda q: q.tensor_copy(out[0], win[0].indirect(off[0])), [out], [win, off])
-        else:
-            add("S", lambda q: q.activation(out[0], win[0].indirect(off[0]), AF.Copy), [out], [win, off])
+            add("S", lambda q: q.activation(out[0], src, AF.Copy), [out], ins)
 
     def tt_(out, a, b, op):
         add("V", lambda q: q.tensor_tensor(out[0], a[0], b[0], op), [out], [a, b])
@@ -118,12 +104,8 @@ def rank_program(g, core, T, topo):
 
     def ts(out, a, s1, op0, s2=None, op1=None):
         ins = [a] + [s for s in (s1, s2) if isinstance(s, tuple)]
-        x1 = s1[0] if isinstance(s1, tuple) else s1
-        x2 = s2[0] if isinstance(s2, tuple) else s2
-        if op1 is None:
-            add("V", lambda q: q.tensor_scalar(out[0], a[0], x1, None, op0), [out], ins)
-        else:
-            add("V", lambda q: q.tensor_scalar(out[0], a[0], x1, x2, op0, op1), [out], ins)
+        x = [s[0] if isinstance(s, tuple) else s for s in (s1, s2)] + [op0] + ([] if op1 is None else [op1])
+        add("V", lambda q: q.tensor_scalar(out[0], a[0], *x), [out], ins)
 
     def tr(out, in_):
         add("V", lambda q: q.transpose(out[0], in_[0]), [out], [in_])
@@ -135,10 +117,8 @@ def rank_program(g, core, T, topo):
         p0, p1 = out[1][1], out[1][2]
         after = [i for i, a, b in pool if a != p0 and a < p1 and p0 < b]
         pool.append((len(ops), p0, p1))
-        if flt:
-            add("G", lambda q: q.iota(out[0], pat, base, cm, allow_small_or_imprecise_dtypes=True), [out], [], after=after)
-        else:
-            add("G", lambda q: q.iota(out[0], pat, base, cm), [out], [], after=after)
+        kw = {"allow_small_or_imprecise_dtypes": True} if flt else {}
+        add("G", lambda q: q.iota(out[0], pat, base, cm, **kw), [out], [], after=after)
 
     def quant(qn, sn, tn, n, c0=0, o0=0):
         a, b, c = v(qn, o0, o0 + n), v(sn, o0, o0 + n), v(tn, 4 * c0, 4 * (c0 + n))
@@ -153,24 +133,26 @@ def rank_program(g, core, T, topo):
         rid, pid, _ = topo.addr(cores[k])
         return DstId(rid=rid, pnc=pid)
 
-    def send_all(src, land, sem):
-        es = topo.engines(core, cores[others[0]])
+    def send_all(src, land, sem, ks):
+        es = topo.engines(core, cores[ks[0]])
         add("G", lambda q: q.remote_dma_fused([RemoteDMATransfer(
-            dst_ids=[dst(k) for k in others], dma_engine_mask=_mask(es), remote_sem=T.sem[sem],
-            srcs=[src[0]], dsts=[land[0] for k in others])], local_sem=T.sem.sent), [], [src], "sent", len(es))
+            dst_ids=[dst(k) for k in ks], dma_engine_mask=_mask(es), remote_sem=T.sem[sem],
+            srcs=[src[0]], dsts=[land[0] for k in ks])], local_sem=T.sem.sent), [], [src], "sent", len(es))
 
     def n_all(k):
         return len(topo.engines(cores[k], core))
 
-    def send_each(srcs, lands, which, sem):
-        plan = _split(topo, cores, r)
-        trs = [RemoteDMATransfer(dst_ids=[dst(p[0])], dma_engine_mask=_mask(p[which]), remote_sem=T.sem[sem],
-                                 src=s[0], dst=l[0]) for p, s, l in zip(plan, srcs, lands)]
-        add("G", lambda q: q.remote_dma_fused(trs, local_sem=T.sem.sent), [], srcs, "sent", sum(len(p[which]) for p in plan))
+    def send(plan, srcs, lands, sem):
+        trs = [RemoteDMATransfer(dst_ids=[dst(k)], dma_engine_mask=_mask(es), remote_sem=T.sem[sem], src=s[0], dst=l[0])
+               for (k, es), s, l in zip(plan, srcs, lands)]
+        add("G", lambda q: q.remote_dma_fused(trs, local_sem=T.sem.sent), [], srcs, "sent", sum(len(es) for k, es in plan))
 
-    def send_tiles(sq, sp, lq, lp, place, sem):
-        send_each([u8(v(sq, 96 * k, 96 * k + 96)) for k in others], [u8(v(lq, place(k), place(k) + 96)) for k in others], 1, sem)
-        send_each([v(sp, 96 * k, 96 * k + 96) for k in others], [v(lp, place(k), place(k) + 96) for k in others], 2, sem)
+    def thirds(which):
+        return [(p[0], p[which]) for p in _split(topo, cores, r)]
+
+    def send_tiles(a, b, place, sem):
+        for which, x, f in ((1, "q", u8), (2, "p", lambda y: y)):
+            send(thirds(which), [f(v(a % x, 96 * k, 96 * k + 96)) for k in others], [f(v(b % x, place(k), place(k) + 96)) for k in others], sem)
 
     def n_each(k, which):
         return [len(p[which]) for p in _split(topo, cores, k) if p[0] == r][0]
@@ -187,7 +169,8 @@ def rank_program(g, core, T, topo):
         for e in range(2):
             p = 32 * q + 16 * e
             dma("SY"[e], v("scraw", 0, 54, 1, p, p + 16), hbm(T.sc[:, 24 * e + 6 * q:24 * e + 6 * q + 54]), "dsc")
-    dma("Y", v("xt0", 0, 4 * C), hbm(T.x[:, :]), "dx")
+    for i in range(3):
+        dma("Y", v("xt0", 512 * i, 512 * i + 512), hbm(T.x[:, 512 * i:512 * i + 512]), "dx%d" % i)
     dma("S", v("ut", 0, 512), hbm(T.u[:, :]), "du")
     for k in range(4):
         for q in range(4):
@@ -203,83 +186,84 @@ def rank_program(g, core, T, topo):
     mset(v("et", 0, 2048), 0.0)
     for i, m in enumerate((96, 112, 32, 64)):
         ts(v("pint", 1 + i, 2 + i), v("pint", 0, 1), m, ALU.bitwise_and)
-    mset(v("aa", 0, 2 * C), 0.0)
-    copy("V", v("col", 4, 8), v("pint", 1, 5))
+    copy("S", v("aa", 0, M), v("et", 512, 2048))
     ts(v("et", 0, 512, 4), v("idm", 0, 128), 0.0, ALU.is_equal)
+    copy("V", v("col", 4, 8), v("pint", 1, 5))
+    ts(SLOT, v("pint", 1, 2), -12.0, ALU.mult, 3.0 * C, ALU.add)
+    ts(BACK, v("pint", 1, 2), 12.0, ALU.mult, -3.0 * C, ALU.add)
+    ts(v("col", 0, 1), v("pint", 1, 2), 11.0, ALU.mult)
     for b in range(1, 4):
         copy("S", v("et", 512 * b + b, 512 * b + 512, 4), v("et", 0, 512, 4))
-    copy("S", v("aa", 2 * C, M), v("aa", 0, 2 * C))
-    for h in range(2):
-        copy("S", v("ww", 2 * C * h, 2 * C * h + 2 * C), v("aa", 0, 2 * C))
+    for i, m in enumerate((32, 64)):
+        ts(v("sci", 56 * i, 56 * i + 54), v("scraw", 0, 54), m, ALU.bitwise_and)
+    ts(v("sci", 168, 222), v("scraw", 0, 54), 7, ALU.logical_shift_right)
+    ts(v("sci", 112, 166), v("scraw", 0, 54), 31, ALU.bitwise_and)
+    ts(v("scf", 0, 54), v("sci", 0, 54), v("col", 6, 7), ALU.not_equal, 768.0, ALU.mult)
+    ts(v("scf", 56, 110), v("sci", 56, 110), v("col", 7, 8), ALU.not_equal, 384.0, ALU.mult)
+    ts(v("scf", 112, 166), v("sci", 168, 222), 32.0, ALU.mult)
+    mset(v("in2", 0, 32), 0.0)
+    tt_(v("scf", 168, 222), v("scf", 0, 54), v("scf", 56, 110), ALU.add)
+    tt_(v("scf", 224, 278), v("scf", 112, 166), v("sci", 112, 166), ALU.add)
+    tt_(v("bet", 144, 192), v("bet", 0, 48), v("bet", 48, 96), ALU.add)
     for kk in range(2):
         for h in range(2):
-            copy("V", v("sco", 2 * kk + h, 12, 4), v("scraw", 48 * kk + h, 48 * kk + 6, 2))
-    mset(v("so", 0, 208), 0.0)
-    for i, m in enumerate((32, 64, 31)):
-        ts(v("sci", 12 * i, 12 * i + 12), v("sco", 0, 12), m, ALU.bitwise_and)
-    ts(v("sci", 36, 48), v("sco", 0, 12), 7, ALU.logical_shift_right)
-    ts(v("scf", 0, 12), v("sci", 0, 12), v("col", 6, 7), ALU.not_equal, 768.0, ALU.mult)
-    ts(v("scf", 12, 24), v("sci", 12, 24), v("col", 7, 8), ALU.not_equal, 384.0, ALU.mult)
-    ts(v("scf", 24, 36), v("sci", 36, 48), 32.0, ALU.mult)
-    mset(v("wk", 0, 1), -BIG)
-    mset(v("wk", 67, 112, 4), -BIG)
-    tt_(v("scf", 48, 60), v("scf", 0, 12), v("scf", 12, 24), ALU.add)
-    tt_(v("scf", 60, 72), v("scf", 24, 36), v("sci", 24, 36), ALU.add)
-    quant("xq0", "xs0", "xt0", C)
-    tt_(v("scl", 12 * r, 12 * r + 12), v("scf", 48, 60), v("scf", 60, 72), ALU.add)
-    send_all(v("scl", 12 * r, 12 * r + 12), v("scl", 12 * r, 12 * r + 12), "scarr")
+            a = 48 * kk + h
+            tt_(v("scl", 12 * r + 2 * kk + h, 12 * r + 12, 4), v("scf", 168 + a, 174 + a - h, 2), v("scf", 224 + a, 230 + a - h, 2), ALU.add)
+    send_all(v("scl", 12 * r, 12 * r + 12), v("scl", 12 * r, 12 * r + 12), "scarr", others[::-1])
     arrive("scarr", sum(n_all(k) for k in others), [v("scl", 12 * k, 12 * k + 12) for k in others])
+    quant("xq0", "xs0", "xt0", 128)
     quant("uq", "up", "ut", 128)
-    tt_(v("bet", 144, 192), v("bet", 0, 48), v("bet", 48, 96), ALU.add)
-    for i in range(3):
-        mset(v("wk", 64 + i, 112, 4), BIG)
+    for i in (1, 2):
+        quant("xq0", "xs0", "xt0", 128, 128 * i, 128 * i)
     ts(v("bet", 192, 240), v("bet", 144, 192), 1.0 / 3, ALU.mult, 0.5 / 3 - 0.5, ALU.add)
     ts(v("bet", 0, 48), v("bet", 144, 192), 32.0, ALU.mult, v("col", 4, 5), ALU.subtract)
+    if r == 0:
+        ts(v("lf", 0, 24, 2), v("i12", 0, 12), v("col", 0, 1), ALU.add)
+    copy("V", v("beti", 0, 48), v("bet", 192, 240))
+    tt_(v("bet", 48, 96), v("bet", 0, 48), v("bet", 96, 144), ALU.add)
+    copy("S", v("ww", 2 * C, M), v("aa", 0, 2 * C))
+    copy("S", v("so", 0, 224), v("aa", 0, 224))
+    for a, b, st, val in ((0, 1, 1, -BIG), (67, 112, 4, -BIG), (64, 112, 4, BIG), (65, 112, 4, BIG), (66, 112, 4, BIG)):
+        o, i = v("wk", a, b, st), v("idm", 0, len(range(a, b, st)))
+        add("S", lambda q, o=o, i=i, val=val: q.activation(o[0], i[0], AF.Identity, bias=val, scale=0.0), [o], [i])
 
     def late_setup():
-        copy("V", v("beti", 0, 48), v("bet", 192, 240))
-        tt_(v("bet", 48, 96), v("bet", 0, 48), v("bet", 96, 144), ALU.add)
-        ts(SLOT, v("pint", 1, 2), -12.0, ALU.mult, 3.0 * C, ALU.add)
-        ts(BACK, v("pint", 1, 2), 12.0, ALU.mult, -3.0 * C, ALU.add)
         ts(v("bet", 240, 288), v("beti", 0, 48), 288.0, ALU.mult)
         quant("pq0", "pp0", "sh0", C)
         for e in range(2):
             tt_(v("aa", 16 * e + 1, M, 32), v("bet", 48, 96), v("bet", 240, 288), ALU.add)
-        ts(v("col", 0, 1), v("pint", 1, 2), 11.0, ALU.mult)
         quant("eq", "ep", "et", 512)
-        if r == 0:
-            ts(v("lf", 0, 24, 2), v("i12", 0, 12), v("col", 0, 1), ALU.add)
 
     def late_loads():
         dma("Y", u8(v("wq", 0, 512)), hbm(T.wc[:, :]), "dw")
         dma("Y", v("wp", 0, 512), hbm(T.ws[:, :]), "dw")
+        dma("Y", v("vt", 0, 512), hbm(T.v[:, :]), "dv")
         for t in range(ROUNDS):
             for c0 in (96, 320):
                 dma("Y", u8(v("mq%d" % t, c0, c0 + 32)), u8(v("xq0", 0, 32)), "dpad")
                 dma("Y", v("mp%d" % t, c0, c0 + 32), v("xs0", 0, 32), "dpad")
-        dma("Y", v("vt", 0, 512), hbm(T.v[:, :]), "dv")
 
-    def lay_table(s):
-        def shift(ds):
-            def f():
-                for d in ds:
-                    a, b = max(0, -32 * d), min(128, 128 - 32 * d)
-                    dma("Y", tabv(None, C * (3 + d), C * (4 + d), a, b), tabv(None, 3 * C, 4 * C, a + 32 * d, b + 32 * d), "drep" + s)
-            return f
-        return [shift((1, -1)), shift((2, 3)), shift((-2, -3))]
+    def lay(s, ds):
+        def f():
+            for d in ds:
+                p0, p1 = max(0, -32 * d), min(128, 128 - 32 * d)
+                dma("Y", tabv(None, C * (3 + d), C * (4 + d), p0, p1), tabv(None, 3 * C, 4 * C, p0 + 32 * d, p1 + 32 * d), "drep" + s)
+        return f
 
-    def spread(src, runs, s0, e1, e2):
+    def spread(src, runs, s0, engs):
         for m0, m1 in runs:
             for e in range(2):
-                copy(e1[e], v("aa", 32 * m0 + 16 * e, 32 * m1, 32), v(src, m0 - s0, m1 - s0))
+                copy(engs[e], v("aa", 32 * m0 + 16 * e, 32 * m1, 32), v(src, m0 - s0, m1 - s0))
                 for a, b in ((0, 64), (64, 0)):
-                    copy(e1[e], v("aa", C + 32 * m0 + 16 * e, C + 32 * m1, 32, a, a + 64), v(src, m0 - s0, m1 - s0, 1, b, b + 64))
-        for q in range(4):
-            o = 32 * (q ^ 1)
-            copy(e2, v("aa", 2 * C, 4 * C, 16, 32 * q, 32 * q + 32), v("aa", 0, 2 * C, 16, o, o + 32))
+                    copy(engs[e], v("aa", C + 32 * m0 + 16 * e, C + 32 * m1, 32, a, a + 64), v(src, m0 - s0, m1 - s0, 1, b, b + 64))
 
-    def rows(runs):
-        for x in range(4):
+    def beside(eng, qs):
+        for q in qs:
+            o = 32 * (q ^ 1)
+            copy(eng, v("aa", 2 * C, 4 * C, 16, 32 * q, 32 * q + 32), v("aa", 0, 2 * C, 16, o, o + 32))
+
+    def rows(runs, xs):
+        for x in xs:
             for m0, m1 in runs:
                 tr(v("ww", M + C * x + 32 * m0, M + C * x + 32 * m1), v("aa", C * x + 32 * m0, C * x + 32 * m1))
 
@@ -298,54 +282,66 @@ def rank_program(g, core, T, topo):
                 copy(e, v("sh" + s, 384 * k, 384 * k + 384, 1, 32 * q, 32 * q + 32), v(X, 384 * q, 384 * q + 384, 1, 32 * k, 32 * k + 32))
         shuf("S", shuffle[:3])
         shuf("V", shuffle[3:5])
-        for i in range(1 if t else 0, 3):
-            mm(i, XQ, XS, 128 * i, "uq", "up", 0, 128)
-        copy("V", v("ssend" + s, 0, 3), v("ps", 0, 1536, 512))
-        send_all(v("ssend" + s, 0, 3), v("sland" + s, 3 * r, 3 * r + 3), "sarr" + s)
+        for i in range(2 if t else 0, 3):
+            mm(4 + i, XQ, XS, 128 * i, "uq", "up", 0, 128)
+        copy("V", v("ssend" + s, 0, 3), v("ps", 2048, 3584, 512))
+        for ks in ([others[::-1]] if last else [others[-1:], others[-2::-1]]):
+            send_all(v("ssend" + s, 0, 3), v("sland" + s, 3 * r, 3 * r + 3), "sarr" + s, ks)
         arrive("sarr" + s, sum(n_all(k) for k in others), [v("sland" + s, 3 * k, 3 * k + 3) for k in others])
         shuf("V", shuffle[5:])
         if t == 0:
             late_setup()
         else:
             quant("pq" + s, "pp" + s, "sh" + s, C)
-        send_tiles("pq" + s, "pp" + s, "lq" + s, "lp" + s, lambda k: 96 * r, "p1arr" + s)
+        send_tiles("p%s" + s, "l%s" + s, lambda k: 96 * r, "p1arr" + s)
         dma("Y", u8(v("lq" + s, 96 * r, 96 * r + 96)), u8(v("pq" + s, 96 * r, 96 * r + 96)), "dp1" + s)
         dma("Y", v("lp" + s, 96 * r, 96 * r + 96), v("pp" + s, 96 * r, 96 * r + 96), "dp1" + s)
         arrive("p1arr" + s, sum(n_tiles(k) for k in others),
                [v(n + s, 96 * k, 96 * k + 96) for k in others for n in ("lq", "lp")])
-        spread("ssend" + s, [(3 * r, 3 * r + 3)], 3 * r, "SS", "S")
-        rows([(3 * r, 3 * r + 3)])
+        spread("ssend" + s, [(3 * r, 3 * r + 3)], 3 * r, "SS")
+        beside("S", range(4))
+        rows([(3 * r, 3 * r + 3)], range(4))
         if t == 0:
             for h in range(2):
                 for x in range(4):
                     copy("V", v("lsc", 4 * h + x, 48, 8), v("scl", 24 * h + x, 24 + 24 * h, 4))
         far = [x for x in ((0, 3 * r), (3 * r + 3, 12)) if x[0] < x[1]]
-        spread("sland" + s, far, 0, "VS", "S")
-        rows(far)
+        spread("sland" + s, far, 0, "VS")
+        beside("S", range(3))
+        rows(far, (0,))
+        beside("V", (3,))
+        rows(far, (1, 2, 3))
+        if t == 0:
+            copy("S", v("ww", 0, 2 * C), v("aa", 0, 2 * C))
         cuts = (("V", 0, 10), ("S", 20, 32), ("V", 10, 20), ("S", 32, 48))
         for e, a, b in cuts:
-            gather(e, v("g0", 16 * a, 16 * b), v("ww", M, 2 * M), v("lsc", a, b))
+            copy(e, v("g0", 16 * a, 16 * b), v("ww", M, 2 * M), v("lsc", a, b))
         for e, a, b in cuts:
             tr(v("tt", 16 * a, 16 * b), v("g0", 16 * a, 16 * b))
-        SC, NB = v("tt", 0, 768, 16), v("tt", 1, 768, 16)
-        scan(v("wk", 1, 49), SC, v("wk", 64, 112), -BIG, ALU.max, ALU.min)
-        tt_(v("wk", 192, 240), SC, v("wk", 0, 48), ALU.is_gt)
-        tt_(v("wk", 128, 176), SC, v("wk", 0, 48), ALU.is_le)
-        tt_(v("wk", 256, 304), v("wk", 192, 240), NB, ALU.mult)
-        scan(v("so", 0, HC, 4), v("wk", 128, 176), v("wk", 256, 304), 0.0, ALU.mult, ALU.add)
-        tr(v("gs", 0, HC), v("so", 12, 12 + HC))
-        publish(0, s, "YS")
-        copy("V", v("lf", 1, 24, 2) if r == 0 else v("la", 0, 12), v("so", 12, 12 + HC, 16))
+        two = ((0, 32, 0), (32, 48, 16))
+        for a, b, o in two:
+            scan(v("wk", 1 + a, 1 + b), v("tt", 16 * a, 16 * b, 16), v("wk", 64 + a, 64 + b), -BIG, ALU.max, ALU.min)
         if t == 0:
-            mset(v("in2", 0, 32), 0.0)
+            for k in range(3):
+                tt_(v("wk", 256 + k, 304, 4), v("tt", 16 * k + 1, 768, 64), v("tt", 16 * k + 17, 768, 64), ALU.subtract)
+            copy("S", v("wk", 259, 304, 4), v("tt", 49, 768, 64))
+        for a, b, o in two:
+            tt_(v("wk", 128 + a, 128 + b), v("tt", 16 * a, 16 * b, 16), v("wk", a, b), ALU.is_le)
+        for a, b, o in two:
+            scan(v("so", 4 * a + o, 4 * b + o, 4), v("wk", 128 + a, 128 + b), v("wk", 256 + a, 256 + b), 0.0, ALU.mult, ALU.add)
+        for a, b, o in two:
+            tr(v("gs", 4 * a, 4 * b), v("so", 4 * a + o + 12, 4 * b + o + 12))
+        publish(0, s, "YS")
+        for a, b, o in two:
+            copy("V", v("lf", a // 2 + 1, b // 2, 2) if r == 0 else v("la", a // 4, b // 4), v("so", 4 * a + o + 12, 4 * b + o, 16))
         for b in range(4):
             mm(4 + b, "eq", "ep", 128 * b, "lq" + s, "lp" + s, 0, C)
         for b in range(4):
-            copy("VSVS"[b], tabv(b, 3 * C, 4 * C), v("ps", 512 * (4 + b), 512 * (4 + b) + C))
-        lay = lay_table(s)
+            copy("SVVV"[b], tabv(b, 3 * C, 4 * C), v("ps", 512 * (4 + b), 512 * (4 + b) + C))
         late = [late_loads] if t == 0 else []
-        after = ({0: lay + late}, {0: lay[:1], 2: lay[1:] + late}, {0: lay[:1], 2: lay[1:2], 4: lay[2:], 6: late},
-                 {0: lay[:1], 2: lay[1:2], 4: lay[2:], 10: late})[r]
+        lays = [lay(s, ds) for ds in ((1,), (-1,), (2, 3), (-2, -3))]
+        after = ({0: lays + late}, {0: lays[:2], 2: lays[2:] + late}, {0: lays[:1], 2: lays[1:2], 4: lays[2:3], 6: lays[3:] + late},
+                 {0: lays[:1], 2: lays[1:2], 4: lays[2:3], 6: lays[3:], 10: late})[r]
         for f in after[0]:
             f()
         for st in range(1, 4 * r + 1):
@@ -354,52 +350,67 @@ def rank_program(g, core, T, topo):
             pub = st % 2 == 0 and j < 2 * r
             src = HC * j if pub else 0
             for h in range(3):
-                gather("S", v("gs", src + 64 * h, src + 64 * h + 64), v("ww", M * w, M * w + M), v("la", 4 * h, 4 * h + 4))
+                copy("S", v("gs", src + 64 * h, src + 64 * h + 64), v("ww", M * w, M * w + M), v("la", 4 * h, 4 * h + 4))
             if pub:
                 publish(j, s, "Y")
             for h in range(4):
                 if h < 3:
                     tr(v("ts", 64 * h, 64 * h + 64), v("gs", src + 64 * h, src + 64 * h + 64))
-                if h > 0:
-                    a = v("ts", 64 * h - 64, 64 * h, 16)
-                    if st == 4 * r:
-                        ts(v("lf", 8 * h - 7, 8 * h, 2), a, float(M), ALU.add)
-                    else:
-                        copy("V", v("la", 4 * h - 4, 4 * h), a)
-                    if st == 4 * r - 2:
-                        copy("V", v("lf", 8 * h - 8, 8 * h, 2), a)
+                if h > 0 and st == 4 * r:
+                    ts(v("lf", 8 * h - 7, 8 * h, 2), v("ts", 64 * h - 64, 64 * h, 16), float(M), ALU.add)
+                elif h > 0:
+                    copy("V", v("la", 4 * h - 4, 4 * h), v("ts", 64 * h - 64, 64 * h, 16))
+            if st == 4 * r - 2:
+                copy("V", v("lf", 0, 24, 2), v("ts", 0, HC, 16))
             for f in after.get(st, []):
                 f()
         for h in range(3):
-            gather("SSV"[h], v("gf", 128 * h, 128 * h + 128), v("ww", 0, 2 * M), v("lf", 8 * h, 8 * h + 8))
+            copy("SVS"[h], v("gf", 128 * h, 128 * h + 128), v("ww", 0, 2 * M), v("lf", 8 * h, 8 * h + 8))
         for h in range(3):
             tr(v("tf", 128 * h, 128 * h + 128), v("gf", 128 * h, 128 * h + 128))
-        for x in range(4):
-            ts(v("ld", 12 * (x // 2) + x % 2, 12 * (x // 2) + 12, 2), v("tf", 16 * x, C, 64), SLOT, ALU.add)
-        n1 = 18 if r == N - 1 else 24
+        for i, k in enumerate(order):
+            for e in range(2):
+                c0 = HC * (k % 2) + 32 * (k // 2) + 16 * e
+                ts(v("ld", 6 * i + e, 6 * i + 6, 2), v("tf", c0, c0 + 129, 64), SLOT, ALU.add)
 
-        def pick(a, b):
-            for x in (2, 0, 3, 1):
-                gather("VVSS"[x], v("ug" + s, 64 * a + x, 64 * b, 4), tabv(x, 0, TW), v("ld", a, b))
-        pick(0, n1)
-        quant("gq" + s, "gp" + s, "ug" + s, 16 * n1)
-        send_tiles("gq" + s, "gp" + s, "mq" + s, "mp" + s, lambda k: p2place(r, k), "p2arr%d_%d" % (t, r))
+        def pick(a, b, engs="VVSS", xs=(2, 0, 3, 1)):
+            for x in xs:
+                copy(engs[x], v("ug" + s, 64 * a + x, 64 * b, 4), tabv(x, 0, TW), v("ld", a, b))
+
+        def part(blocks, x):
+            f = u8 if x == "q" else (lambda y: y)
+            send([(order[i], es) for i, es in blocks], [f(v("ggb"[i] + x + s, 96 * i, 96 * i + 96)) for i, es in blocks],
+                 [f(v("m" + x + s, 224, 320)) for i, es in blocks], "p2arr%d_%d" % (t, r))
+        if not last:
+            pick(0, 24)
+            quant("gq" + s, "gp" + s, "ug" + s, C)
+            send_tiles("g%s" + s, "m%s" + s, lambda k: p2place(r, k), "p2arr%d_%d" % (t, r))
+        else:
+            es = topo.engines(core, cores[near])
+            h2, h4 = len(es) // 2, len(es) // 4
+            pick(0, 12)
+            pick(12, 18, "VSSS", (2, 3, 1))
+            quant("gq" + s, "gp" + s, "ug" + s, HC)
+            pick(12, 18, "VSSS", (0,))
+            part([(0, es[:h2]), (1, es[h2:])], "q")
+            quant("bq" + s, "bp" + s, "ug" + s, 128, 160, 160)
+            part([(0, es[:h4]), (1, es[h4:h2]), (2, es[h2:])], "p")
+            part([(2, es)], "q")
+            pick(18, 24)
         for k in others:
             c0 = p2place(k, r)
-            arrive("p2arr%d_%d" % (t, k), n_tiles(k), [v(n + s, c0, c0 + 96) for n in ("mq", "mp")])
-        if n1 < 24:
-            pick(n1, 24)
-            quant("oq" + s, "op" + s, "ug" + s, 128, C - 128)
-        fill = []
+            n = n_tiles(k) if k < N - 1 else 3 * n_all(k) // (2 if r == near else 4)
+            arrive("p2arr%d_%d" % (t, k), n, [v(x + s, c0, c0 + 96) for x in ("mq", "mp")])
         if t == 0:
-            quant("vq", "vp", "vt", 128)
+            fill = [lambda: quant("vq", "vp", "vt", 128)]
         else:
             def pl_send():
                 tt_(v("plsend", 0, 24), v("pw", 96, 120), v("pw", 56, 80), ALU.add)
-                send_each([v("plsend", 6 * k, 6 * k + 6) for k in others], [v("pland", 6 * r, 6 * r + 6) for k in others], 2, "plarr")
+                send(thirds(2), [v("plsend", 6 * order.index(k), 6 * order.index(k) + 6) for k in others],
+                     [v("pland", 6 * r, 6 * r + 6) for k in others], "plarr")
                 arrive("plarr", sum(n_each(k, 2) for k in others), [v("pland", 6 * k, 6 * k + 6) for k in others])
-            ts(v("pw", 0, 24), v("ld", 0, 24), BACK, ALU.add)
-            fill = [lambda: (ts(v("pw", 32, 56), v("pw", 0, 24), 1.0 / 96, ALU.mult, 0.5 / 96 - 0.5, ALU.add),
+            fill = [lambda: ts(v("pw", 0, 24), v("ld", 0, 24), BACK, ALU.add),
+                    lambda: (ts(v("pw", 32, 56), v("pw", 0, 24), 1.0 / 96, ALU.mult, 0.5 / 96 - 0.5, ALU.add),
                              ts(v("pw", 56, 80), v("pw", 0, 24), 1.0 / C, ALU.mult, 0.5 / C - 0.5, ALU.add)),
                     lambda: copy("V", v("pwi", 0, 48), v("pw", 32, 80)),
                     lambda: (ts(v("pw", 32, 56), v("pwi", 0, 24), 288.0, ALU.mult),
@@ -408,69 +419,99 @@ def rank_program(g, core, T, topo):
                     pl_send]
         H, HQ, HP = "ht" + s, "hq" + s, "hp" + s
         XN, XQN, XSN = "xt%d" % (t + 1), "xq%d" % (t + 1), "xs%d" % (t + 1)
-        for i, k in enumerate([r] + others if n1 == 24 else others + [r]):
+        for i, k in enumerate(others + [r] if last else [r] + others):
             if k != r:
                 names, c0 = ("mq" + s, "mp" + s), p2place(k, r)
                 lo = 96 if c0 == 128 else c0
-            elif n1 == 24:
+            elif not last:
                 names, c0, lo = ("gq" + s, "gp" + s), 96 * r, 96 * r
             else:
                 names, c0, lo = ("oq" + s, "op" + s), 32, 0
             base = 4 * (i % 2)
             for b in (0, 2, 1, 3):
                 mm(base + b, "eq", "ep", 128 * b, names[0], names[1], lo, 128)
-            for h in range(2):
-                for b in (0, 2, 1, 3):
-                    for q in (2 * h, 2 * h + 1):
+
+            def unpack(engs, bs, qs):
+                for b in bs:
+                    for q in qs:
                         c = 512 * (base + b) + c0 - lo
-                        copy("VVSV"[b] if (h == 1 and i < N - 1) else "VVSS"[b],
-                             v(H, 384 * q + b, 384 * q + 384, 4, 32 * k, 32 * k + 32), v("ps", c, c + 96, 1, 32 * q, 32 * q + 32))
-                if fill:
+                        copy(engs[b], v(H, 384 * q + b, 384 * q + 384, 4, 32 * k, 32 * k + 32), v("ps", c, c + 96, 1, 32 * q, 32 * q + 32))
+            if last and i < 2:
+                for b in (0, 2, 1, 3):
+                    c = 512 * (base + b) + c0 - lo
+                    copy("VVSS"[b], v("hs" + s, 384 * i + b, 384 * i + 384, 4), v("ps", c, c + 96))
+                for q in range(4):
+                    dma("Y", v(H, 384 * q, 384 * q + 384, 1, 32 * k, 32 * k + 32),
+                        v("hs" + s, 384 * i, 384 * i + 384, 1, 32 * q, 32 * q + 32), "dh" + s)
+                if i == 0:
+                    quant("oq" + s, "op" + s, "ug" + s, 128, 256)
+                else:
                     fill.pop(0)()
-                if i == N - 1:
-                    quant(HQ, HP, H, HC, HC * h, HC * h)
+            elif i < N - 1:
+                for h in range(2):
                     for b in (0, 2, 1, 3):
-                        mm(4 * h + b, "wq", "wp", 128 * b, HQ, HP, HC * h, HC)
-        for h in range(2):
-            for b in (0, 2, 1, 3):
-                o, a = v(XN, 4 * HC * h + b, 4 * HC * (h + 1), 4), v("ps", 512 * (4 * h + b), 512 * (4 * h + b) + HC)
+                        unpack(("VVSS", "VVSV")[h], (b,), (2 * h, 2 * h + 1))
+                        if fill and (b == 3 or (last and b < 2)):
+                            fill.pop(0)()
+            else:
+                unpack("VVSV", (0, 2, 1, 3), (0, 1))
+                unpack("VVSS", (2, 0, 1), (2,))
+                unpack("VVSS", (2,), (3,))
+                quant(HQ, HP, H, 128)
+                unpack("VVSS", (3,), (2, 3))
+                unpack("VVSS", (0, 1), (3,))
+                quant(HQ, HP, H, 128, 128, 128)
+                quant(HQ, HP, H, 128, 256, 256)
+
+        def layer(h):
+            for b in (2, 0, 3, 1):
+                mm(4 * (h % 2) + b, "wq", "wp", 128 * b, HQ, HP, 128 * h, 128)
+        layer(0)
+        layer(1)
+        for h in range(3):
+            for b in (2, 0, 3, 1):
+                o, a = v(XN, 512 * h + b, 512 * (h + 1), 4), v("ps", 512 * (4 * (h % 2) + b), 512 * (4 * (h % 2) + b) + 128)
                 if b < 2:
                     ts(o, a, 0.0, ALU.max, 0.03125, ALU.mult)
                 else:
                     add("S", lambda q, o=o, a=a: q.activation(o[0], a[0], AF.Relu, scale=0.03125), [o], [a])
-            quant(XQN, XSN, XN, HC, HC * h, HC * h)
-            if t < ROUNDS - 1 and h == 0:
-                mm(0, XQN, XSN, 0, "uq", "up", 0, 128)
+            if h == 0:
+                layer(2)
+            if t == ROUNDS - 1 and h == 2:
+                copy("V", v("in2", 6 * r, 6 * r + 6), v("plsend", 6 * r, 6 * r + 6))
+                for a, b in ((0, 6 * r), (6 * r + 6, 24)):
+                    if a < b:
+                        copy("V", v("in2", a, b), v("pland", a, b))
+            quant(XQN, XSN, XN, 128, 128 * h, 128 * h)
+            if t < ROUNDS - 1 and h == 1:
+                for x in range(2):
+                    mm(4 + x, XQN, XSN, 128 * x, "uq", "up", 0, 128)
                 for k in range(4):
                     for q in range(2):
                         dma("Y", v("sh1", 384 * k, 384 * k + 384, 1, 32 * q, 32 * q + 32),
                             v(XN, 384 * q, 384 * q + 384, 1, 32 * k, 32 * k + 32), "dsh1")
-            if t == ROUNDS - 1:
-                if h == 0:
-                    copy("V", v("in2", 6 * r, 6 * r + 6), v("plsend", 6 * r, 6 * r + 6))
-                dma("Y", hbm(T.oc[:, 4 * HC * h:4 * HC * (h + 1)]), u8(v("xq2", HC * h, HC * h + HC)), "doc")
+            if t == ROUNDS - 1 and h == 1:
+                mm(4, "vq", "vp", 0, "xq2", "xs2", 0, 256)
+                dma("Y", hbm(T.oc[:, 0:1024]), u8(v("xq2", 0, 256)), "doc")
 
-    for h in range(2):
-        mm(h, "vq", "vp", 0, "xq2", "xs2", HC * h, HC)
-    for a, b in ((0, 6 * r), (6 * r + 6, 24)):
-        if a < b:
-            copy("V", v("in2", a, b), v("pland", a, b))
-    copy("S", v("ysb", 0, HC), v("ps", 0, HC))
+    mm(5, "vq", "vp", 0, "xq2", "xs2", 256, 128)
     tr(v("plt", 0, 32), v("in2", 0, 32))
-    dma("S", hbm(T.y[:, 0:HC]), v("ysb", 0, HC), "dy")
-    copy("V", v("ysb", HC, C), v("ps", 512, 512 + HC))
+    copy("S", v("ysb", 0, 256), v("ps", 2048, 2048 + 256))
+    copy("V", v("ysb", 256, C), v("ps", 2560, 2560 + 128))
+    dma("S", hbm(T.y[:, 0:256]), v("ysb", 0, 256), "dy")
+    dma("Y", hbm(T.oc[:, 1024:4 * C]), u8(v("xq2", 256, C)), "doc")
     for k in range(4):
-        dma("SY"[k % 2], hbm(T.osc[4 * k:4 * k + 4, :]), v("xs2", 0, C, 1, 32 * k, 32 * k + 4), "doc")
+        dma("YS"[k % 2], hbm(T.osc[4 * k:4 * k + 4, :]), v("xs2", 0, C, 1, 32 * k, 32 * k + 4), "doc")
     for q in range(4):
-        dma("S", hbm(T.pl[0:8:2, 96 * q:96 * q + 96]), v("plt", 0, 16, 1, 32 * q, 32 * q + 24), "dpl")
-        if q == 1:
-            dma("Y", hbm(T.y[:, HC:C]), v("ysb", HC, C), "dy")
-        dma("Y", hbm(T.pl[1:8:2, 96 * q:96 * q + 96]), v("plt", 16, 32, 1, 32 * q, 32 * q + 24), "dpl")
+        for e in range(2):
+            if (q, e) == (3, 1):
+                dma("Y", hbm(T.y[:, 256:C]), v("ysb", 256, C), "dy")
+            dma("SY"[e], hbm(T.pl[e:8:2, 96 * q:96 * q + 96]), v("plt", 16 * e, 16 * e + 16, 1, 32 * q, 32 * q + 24), "dpl")
 
     def meet(a, b):
         return a[0] == b[0] and a[1] < b[2] and b[1] < a[2] and not a[3].isdisjoint(b[3])
 
-    seen = {}
+    seen, need, count, waited = {}, set(), {}, {}
     for i, op in enumerate(ops):
         deps = set(op["a"])
         for regs, mine in ((op["w"], True), (op["r"], False)):
@@ -482,34 +523,26 @@ def rank_program(g, core, T, topo):
                     if clash and j != i and meet(reg, other):
                         deps.add(j)
         op["d"] = set() if op["e"] == "X" else deps
-        for reg in op["w"]:
-            seen.setdefault(reg[0], []).append((i, reg, True))
-        for reg in op["r"]:
-            seen.setdefault(reg[0], []).append((i, reg, False))
-    need = set()
+        for regs, mine in ((op["w"], True), (op["r"], False)):
+            for reg in regs:
+                seen.setdefault(reg[0], []).append((i, reg, mine))
     for op in ops:
-        last = {}
+        latest = {}
         for j in op["d"]:
             if ops[j]["sem"] is None:
-                last[ops[j]["e"]] = max(last.get(ops[j]["e"], -1), j)
-        op["last"] = last
-        need.update(last.values())
-    count = {}
+                latest[ops[j]["e"]] = max(latest.get(ops[j]["e"], -1), j)
+        op["last"] = latest
+        need.update(latest.values())
     for i, op in enumerate(ops):
         if op["sem"] is None and i in need:
             count[op["e"]] = count.get(op["e"], 0) + 1
             op["n"] = count[op["e"]]
-    waited = {}
     for i, op in enumerate(ops):
         if op["e"] == "X":
             continue
         q = queue[op["e"]]
-        want = {}
-        for e, j in op["last"].items():
-            want["c" + e] = ops[j]["n"]
-        for j in op["d"]:
-            if ops[j]["sem"] is not None:
-                want[ops[j]["sem"]] = total[ops[j]["sem"]]
+        want = {"c" + e: ops[j]["n"] for e, j in op["last"].items()}
+        want.update({ops[j]["sem"]: total[ops[j]["sem"]] for j in op["d"] if ops[j]["sem"] is not None})
         for name in sorted(want):
             if waited.get((op["e"], name), 0) < want[name]:
                 q.wait_ge(T.sem[name], want[name])

from concourse.bass import DstId, RemoteDMATransfer
from concourse.mybir import dt, AluOpType as ALU, ActivationFunctionType as AF

N, C, ROUNDS = 4, 384, 2
M = N * C
HC = C // 2
TW = 7 * C
BIG = 1e29
F32, BF, I32, U16, CODE, U8 = "float32", "bfloat16", "int32", "uint16", "float8_e4m3fn_x4", "uint8"

SCRATCH = {"ps": ("psum", [128, 4096], F32), "tab": ("sbuf", [128, 4, TW], BF)}


def _sb(d, **names):
    for name, n in names.items():
        SCRATCH[name] = ("sbuf", [128, n], d)


for _t in range(ROUNDS):
    for _n, _w in (("p", C), ("l", C), ("g", C), ("b", C), ("o", 128), ("m", 352), ("h", C)):
        _sb(CODE, **{"%sq%d" % (_n, _t): _w}); _sb(U8, **{"%sp%d" % (_n, _t): _w})
    _sb(BF, **{"sh%d" % _t: M, "ug%d" % _t: M, "ht%d" % _t: M, "hs%d" % _t: 2 * C})
    _sb(F32, **{"ssend%d" % _t: 4, "sland%d" % _t: 12})
_sb(BF, xt0=M, xt1=M, xt2=M, ut=512, vt=512, et=2048)
_sb(CODE, xq0=C, xq1=C, xq2=C, uq=128, vq=128, wq=512, eq=512)
_sb(U8, xs0=C, xs1=C, xs2=C, up=128, vp=128, wp=512, ep=512)
_sb(F32, ww=2 * M, aa=M, g0=768, tt=768, gs=6 * HC, ts=HC, gf=C, tf=C, bet=288, scf=280, scl=48, wk=320, so=224, idm=128,
    i12=12, col=8, pw=128, ysb=C, plsend=24, pland=24, in2=32, plt=32)
_sb(I32, beti=48, scraw=56, sci=224, pint=8, pwi=48)
_sb(U16, lsc=48, la=12, lf=24, ld=24)

SEMAPHORES = ["cV", "cS", "cT", "cG", "sent", "scarr", "plarr", "dx0", "dx1", "dx2", "du", "dsc", "dsh0", "dsh1",
              "dw", "dv", "dpad", "dy", "doc", "dpl"]
for _t in range(ROUNDS):
    SEMAPHORES += ["sarr%d" % _t, "p1arr%d" % _t, "dp1%d" % _t, "drep%d" % _t, "dh%d" % _t]
    SEMAPHORES += ["p2arr%d_%d" % (_t, _k) for _k in range(N)] + ["dpub%d_%d" % (_t, _k) for _k in range(6)]


def _split(topo, cores, r):
    o = [k for k in range(N) if k != r]
    e = topo.engines(cores[r], cores[o[0]])
    h, q = len(e) // 2, len(e) // 4
    return [(o[0], e[:q], e[h:h + q]), (o[1], e[q:h], e[h + q:]), (o[2], e[h:], e[:h])]


def _mask(es):
    return sum(1 << e for e in es)


def rank_program(g, core, T, topo):
    r = T.rank_of(core)
    if r is None:
        return
    cores = T.cores
    others = [k for k in range(N) if k != r]
    last = r == N - 1
    near = ([k for k in range(N - 1) if topo.same_plane(topo.chip(cores[k]), topo.chip(cores[-1]))] + [N - 2])[0]
    order = [k for k in range(N - 1) if k != near] + [near, N - 1] if last else list(range(N))
    queue = {"V": g.vector, "S": g.scalar, "T": g.tensor, "G": g, "Y": g.sync}
    ops, total, pool = [], {}, []

    def v(name, c0, c1, step=1, p0=0, p1=128, ps=1):
        rows = slice(p0, p1, ps) if ps != 1 else slice(p0, p1)
        ap = T[name][rows, c0:c1:step] if step != 1 else T[name][rows, c0:c1]
        if name == "ps":
            return (ap, (name, 0, 128, frozenset(c // 512 for c in range(c0, c1, step))))
        return (ap, (name, p0, p1, frozenset(range(c0, c1, step))))

    def tabv(b, c0, c1, p0=0, p1=128):
        bs = range(4) if b is None else [b]
        ap = T.tab[p0:p1, :, c0:c1] if b is None else T.tab[p0:p1, b, c0:c1]
        return (ap, ("tab", p0, p1, frozenset(7 * x + s for x in bs for s in range(c0 // C, c1 // C))))

    def u8(x):
        return (x[0].bitcast(dt.uint8), x[1])

    def add(eng, fn, outs, ins, sem=None, inc=0, after=()):
        ops.append({"e": eng, "f": fn, "w": [o[1] for o in outs], "r": [i[1] for i in ins], "sem": sem, "a": set(after)})
        if sem is not None:
            total[sem] = total.get(sem, 0) + inc

    def arrive(sem, inc, outs):
        add("X", None, outs, [], sem, inc)

    def dma(eng, out, in_, sem):
        add(eng, lambda q: q.dma_start(out[0], in_[0]), [out] if out[1] else [], [in_] if in_[1] else [], sem, 16)

    def hbm(ap):
        return (ap, None)

    def copy(eng, out, in_, off=None):
        src = in_[0] if off is None else in_[0].indirect(off[0])
        ins = [in_] if off is None else [in_, off]
        if eng == "V":
            add("V", lambda q: q.tensor_copy(out[0], src), [out], ins)
        else:
            add("S", lambda q: q.activation(out[0], src, AF.Copy), [out], ins)

    def tt_(out, a, b, op):
        add("V", lambda q: q.tensor_tensor(out[0], a[0], b[0], op), [out], [a, b])

    def scan(out, a, b, first, op0, op1):
        add("V", lambda q: q.tensor_tensor_scan(out[0], a[0], b[0], first, op0, op1), [out], [a, b])

    def ts(out, a, s1, op0, s2=None, op1=None):
        ins = [a] + [s for s in (s1, s2) if isinstance(s, tuple)]
        x = [s[0] if isinstance(s, tuple) else s for s in (s1, s2)] + [op0] + ([] if op1 is None else [op1])
        add("V", lambda q: q.tensor_scalar(out[0], a[0], *x), [out], ins)

    def tr(out, in_):
        add("V", lambda q: q.transpose(out[0], in_[0]), [out], [in_])

    def mset(out, val):
        add("V", lambda q: q.memset(out[0], val), [out], [])

    def iota(out, pat, base, cm, flt=True):
        p0, p1 = out[1][1], out[1][2]
        after = [i for i, a, b in pool if a != p0 and a < p1 and p0 < b]
        pool.append((len(ops), p0, p1))
        kw = {"allow_small_or_imprecise_dtypes": True} if flt else {}
        add("G", lambda q: q.iota(out[0], pat, base, cm, **kw), [out], [], after=after)

    def quant(qn, sn, tn, n, c0=0, o0=0):
        a, b, c = v(qn, o0, o0 + n), v(sn, o0, o0 + n), v(tn, 4 * c0, 4 * (c0 + n))
        add("V", lambda q: q.quantize_mx(a[0], b[0], c[0]), [a, b], [c])

    def mm(bank, lq, lp, l0, rq, rp, r0, n):
        o = v("ps", 512 * bank, 512 * bank + n)
        a, b, c, d = v(lq, l0, l0 + 128), v(lp, l0, l0 + 128), v(rq, r0, r0 + n), v(rp, r0, r0 + n)
        add("T", lambda q: q.matmul_mx(o[0], a[0], b[0], c[0], d[0], True, True), [o], [a, b, c, d])

    def dst(k):
        rid, pid, _ = topo.addr(cores[k])
        return DstId(rid=rid, pnc=pid)

    def send_all(src, land, sem, ks):
        es = topo.engines(core, cores[ks[0]])
        add("G", lambda q: q.remote_dma_fused([RemoteDMATransfer(
            dst_ids=[dst(k) for k in ks], dma_engine_mask=_mask(es), remote_sem=T.sem[sem],
            srcs=[src[0]], dsts=[land[0] for k in ks])], local_sem=T.sem.sent), [], [src], "sent", len(es))

    def n_all(k):
        return len(topo.engines(cores[k], core))

    def send(plan, srcs, lands, sem):
        trs = [RemoteDMATransfer(dst_ids=[dst(k)], dma_engine_mask=_mask(es), remote_sem=T.sem[sem], src=s[0], dst=l[0])
               for (k, es), s, l in zip(plan, srcs, lands)]
        add("G", lambda q: q.remote_dma_fused(trs, local_sem=T.sem.sent), [], srcs, "sent", sum(len(es) for k, es in plan))

    def thirds(which):
        return [(p[0], p[which]) for p in _split(topo, cores, r)]

    def send_tiles(a, b, place, sem):
        for which, x, f in ((1, "q", u8), (2, "p", lambda y: y)):
            send(thirds(which), [f(v(a % x, 96 * k, 96 * k + 96)) for k in others], [f(v(b % x, place(k), place(k) + 96)) for k in others], sem)

    def n_each(k, which):
        return [len(p[which]) for p in _split(topo, cores, k) if p[0] == r][0]

    def n_tiles(k):
        return n_each(k, 1) + n_each(k, 2)

    def p2place(src, at):
        return (0, 128, 224)[[k for k in range(N) if k != at].index(src)]

    SLOT, BACK = v("col", 2, 3), v("col", 3, 4)

    for q in range(4):
        for e in range(2):
            p = 32 * q + 16 * e
            dma("SY"[e], v("scraw", 0, 54, 1, p, p + 16), hbm(T.sc[:, 24 * e + 6 * q:24 * e + 6 * q + 54]), "dsc")
    for i in range(3):
        dma("Y", v("xt0", 512 * i, 512 * i + 512), hbm(T.x[:, 512 * i:512 * i + 512]), "dx%d" % i)
    dma("S", v("ut", 0, 512), hbm(T.u[:, :]), "du")
    for k in range(4):
        for q in range(4):
            dma("Y", v("sh0", 384 * k, 384 * k + 384, 1, 32 * q, 32 * q + 32),
                hbm(T.x[32 * k:32 * k + 32, 384 * q:384 * q + 384]), "dsh0")
    iota(v("pint", 0, 1), [[0, 1]], 0, 1, False)
    iota(v("idm", 0, 128), [[-1, 128]], 0, 1)
    iota(v("bet", 48, 96), [[0, 16], [4, 3]], 0, 0)
    iota(v("bet", 96, 144), [[0, 4], [96, 4], [0, 3]], 0, 1)
    iota(v("i12", 0, 12), [[32, 6], [192, 2]], 0, 1)
    for q in range(4):
        iota(v("bet", 0, 48, 1, 32 * q, 32 * q + 32), [[1 - 2 * (q % 2), 2], [2 - 4 * (q // 2), 2], [0, 12]], q, 0)
    mset(v("et", 0, 2048), 0.0)
    for i, m in enumerate((96, 112, 32, 64)):
        ts(v("pint", 1 + i, 2 + i), v("pint", 0, 1), m, ALU.bitwise_and)
    copy("S", v("aa", 0, M), v("et", 512, 2048))
    ts(v("et", 0, 512, 4), v("idm", 0, 128), 0.0, ALU.is_equal)
    copy("V", v("col", 4, 8), v("pint", 1, 5))
    ts(SLOT, v("pint", 1, 2), -12.0, ALU.mult, 3.0 * C, ALU.add)
    ts(BACK, v("pint", 1, 2), 12.0, ALU.mult, -3.0 * C, ALU.add)
    ts(v("col", 0, 1), v("pint", 1, 2), 11.0, ALU.mult)
    for b in range(1, 4):
        copy("S", v("et", 512 * b + b, 512 * b + 512, 4), v("et", 0, 512, 4))
    for i, m in enumerate((32, 64)):
        ts(v("sci", 56 * i, 56 * i + 54), v("scraw", 0, 54), m, ALU.bitwise_and)
    ts(v("sci", 168, 222), v("scraw", 0, 54), 7, ALU.logical_shift_right)
    ts(v("sci", 112, 166), v("scraw", 0, 54), 31, ALU.bitwise_and)
    ts(v("scf", 0, 54), v("sci", 0, 54), v("col", 6, 7), ALU.not_equal, 768.0, ALU.mult)
    ts(v("scf", 56, 110), v("sci", 56, 110), v("col", 7, 8), ALU.not_equal, 384.0, ALU.mult)
    ts(v("scf", 112, 166), v("sci", 168, 222), 32.0, ALU.mult)
    mset(v("in2", 0, 32), 0.0)
    tt_(v("scf", 168, 222), v("scf", 0, 54), v("scf", 56, 110), ALU.add)
    tt_(v("scf", 224, 278), v("scf", 112, 166), v("sci", 112, 166), ALU.add)
    tt_(v("bet", 144, 192), v("bet", 0, 48), v("bet", 48, 96), ALU.add)
    for kk in range(2):
        for h in range(2):
            a = 48 * kk + h
            tt_(v("scl", 12 * r + 2 * kk + h, 12 * r + 12, 4), v("scf", 168 + a, 174 + a - h, 2), v("scf", 224 + a, 230 + a - h, 2), ALU.add)
    send_all(v("scl", 12 * r, 12 * r + 12), v("scl", 12 * r, 12 * r + 12), "scarr", others[::-1])
    arrive("scarr", sum(n_all(k) for k in others), [v("scl", 12 * k, 12 * k + 12) for k in others])
    quant("xq0", "xs0", "xt0", 128)
    quant("uq", "up", "ut", 128)
    for i in (1, 2):
        quant("xq0", "xs0", "xt0", 128, 128 * i, 128 * i)
    ts(v("bet", 192, 240), v("bet", 144, 192), 1.0 / 3, ALU.mult, 0.5 / 3 - 0.5, ALU.add)
    ts(v("bet", 0, 48), v("bet", 144, 192), 32.0, ALU.mult, v("col", 4, 5), ALU.subtract)
    if r == 0:
        ts(v("lf", 0, 24, 2), v("i12", 0, 12), v("col", 0, 1), ALU.add)
    copy("V", v("beti", 0, 48), v("bet", 192, 240))
    tt_(v("bet", 48, 96), v("bet", 0, 48), v("bet", 96, 144), ALU.add)
    copy("S", v("ww", 2 * C, M), v("aa", 0, 2 * C))
    copy("S", v("so", 0, 224), v("aa", 0, 224))
    for a, b, st, val in ((0, 1, 1, -BIG), (67, 112, 4, -BIG), (64, 112, 4, BIG), (65, 112, 4, BIG), (66, 112, 4, BIG)):
        o, i = v("wk", a, b, st), v("idm", 0, len(range(a, b, st)))
        add("S", lambda q, o=o, i=i, val=val: q.activation(o[0], i[0], AF.Identity, bias=val, scale=0.0), [o], [i])

    def late_setup():
        ts(v("bet", 240, 288), v("beti", 0, 48), 288.0, ALU.mult)
        quant("pq0", "pp0", "sh0", C)
        for e in range(2):
            tt_(v("aa", 16 * e + 1, M, 32), v("bet", 48, 96), v("bet", 240, 288), ALU.add)
        quant("eq", "ep", "et", 512)

    def late_loads():
        dma("Y", u8(v("wq", 0, 512)), hbm(T.wc[:, :]), "dw")
        dma("Y", v("wp", 0, 512), hbm(T.ws[:, :]), "dw")
        dma("Y", v("vt", 0, 512), hbm(T.v[:, :]), "dv")
        for t in range(ROUNDS):
            for c0 in (96, 320):
                dma("Y", u8(v("mq%d" % t, c0, c0 + 32)), u8(v("xq0", 0, 32)), "dpad")
                dma("Y", v("mp%d" % t, c0, c0 + 32), v("xs0", 0, 32), "dpad")

    def lay(s, ds):
        def f():
            for d in ds:
                p0, p1 = max(0, -32 * d), min(128, 128 - 32 * d)
                dma("Y", tabv(None, C * (3 + d), C * (4 + d), p0, p1), tabv(None, 3 * C, 4 * C, p0 + 32 * d, p1 + 32 * d), "drep" + s)
        return f

    def spread(src, runs, s0, engs):
        for m0, m1 in runs:
            for e in range(2):
                copy(engs[e], v("aa", 32 * m0 + 16 * e, 32 * m1, 32), v(src, m0 - s0, m1 - s0))
                for a, b in ((0, 64), (64, 0)):
                    copy(engs[e], v("aa", C + 32 * m0 + 16 * e, C + 32 * m1, 32, a, a + 64), v(src, m0 - s0, m1 - s0, 1, b, b + 64))

    def beside(eng, qs):
        for q in qs:
            o = 32 * (q ^ 1)
            copy(eng, v("aa", 2 * C, 4 * C, 16, 32 * q, 32 * q + 32), v("aa", 0, 2 * C, 16, o, o + 32))

    def rows(runs, xs):
        for x in xs:
            for m0, m1 in runs:
                tr(v("ww", M + C * x + 32 * m0, M + C * x + 32 * m1), v("aa", C * x + 32 * m0, C * x + 32 * m1))

    def publish(j, s, qs):
        for x in range(8):
            dma(qs[x % len(qs)], v("ww", M * (j % 2), M * (j % 2) + M, 1, 16 * x, 16 * x + 1),
                v("gs", HC * j, HC * j + HC, 1, 0, 128, 16), "dpub%s_%d" % (s, j))

    for t in range(ROUNDS):
        s = str(t)
        X, XQ, XS = "xt" + s, "xq" + s, "xs" + s
        shuffle = [(q, k) for k in range(4) for q in (2, 3)] if t else []

        def shuf(e, part):
            for q, k in part:
                copy(e, v("sh" + s, 384 * k, 384 * k + 384, 1, 32 * q, 32 * q + 32), v(X, 384 * q, 384 * q + 384, 1, 32 * k, 32 * k + 32))
        shuf("S", shuffle[:3])
        shuf("V", shuffle[3:5])
        for i in range(2 if t else 0, 3):
            mm(4 + i, XQ, XS, 128 * i, "uq", "up", 0, 128)
        copy("V", v("ssend" + s, 0, 3), v("ps", 2048, 3584, 512))
        for ks in ([others[::-1]] if last else [others[-1:], others[-2::-1]]):
            send_all(v("ssend" + s, 0, 3), v("sland" + s, 3 * r, 3 * r + 3), "sarr" + s, ks)
        arrive("sarr" + s, sum(n_all(k) for k in others), [v("sland" + s, 3 * k, 3 * k + 3) for k in others])
        shuf("V", shuffle[5:])
        if t == 0:
            late_setup()
        else:
            quant("pq" + s, "pp" + s, "sh" + s, C)
        send_tiles("p%s" + s, "l%s" + s, lambda k: 96 * r, "p1arr" + s)
        dma("Y", u8(v("lq" + s, 96 * r, 96 * r + 96)), u8(v("pq" + s, 96 * r, 96 * r + 96)), "dp1" + s)
        dma("Y", v("lp" + s, 96 * r, 96 * r + 96), v("pp" + s, 96 * r, 96 * r + 96), "dp1" + s)
        arrive("p1arr" + s, sum(n_tiles(k) for k in others),
               [v(n + s, 96 * k, 96 * k + 96) for k in others for n in ("lq", "lp")])
        spread("ssend" + s, [(3 * r, 3 * r + 3)], 3 * r, "SS")
        beside("S", range(4))
        rows([(3 * r, 3 * r + 3)], range(4))
        if t == 0:
            for h in range(2):
                for x in range(4):
                    copy("V", v("lsc", 4 * h + x, 48, 8), v("scl", 24 * h + x, 24 + 24 * h, 4))
        far = [x for x in ((0, 3 * r), (3 * r + 3, 12)) if x[0] < x[1]]
        spread("sland" + s, far, 0, "VS")
        beside("S", range(3))
        rows(far, (0,))
        beside("V", (3,))
        rows(far, (1, 2, 3))
        if t == 0:
            copy("S", v("ww", 0, 2 * C), v("aa", 0, 2 * C))
        cuts = (("V", 0, 10), ("S", 20, 32), ("V", 10, 20), ("S", 32, 48))
        for e, a, b in cuts:
            copy(e, v("g0", 16 * a, 16 * b), v("ww", M, 2 * M), v("lsc", a, b))
        for e, a, b in cuts:
            tr(v("tt", 16 * a, 16 * b), v("g0", 16 * a, 16 * b))
        two = ((0, 32, 0), (32, 48, 16))
        for a, b, o in two:
            scan(v("wk", 1 + a, 1 + b), v("tt", 16 * a, 16 * b, 16), v("wk", 64 + a, 64 + b), -BIG, ALU.max, ALU.min)
        if t == 0:
            for k in range(3):
                tt_(v("wk", 256 + k, 304, 4), v("tt", 16 * k + 1, 768, 64), v("tt", 16 * k + 17, 768, 64), ALU.subtract)
            copy("S", v("wk", 259, 304, 4), v("tt", 49, 768, 64))
        for a, b, o in two:
            tt_(v("wk", 128 + a, 128 + b), v("tt", 16 * a, 16 * b, 16), v("wk", a, b), ALU.is_le)
        for a, b, o in two:
            scan(v("so", 4 * a + o, 4 * b + o, 4), v("wk", 128 + a, 128 + b), v("wk", 256 + a, 256 + b), 0.0, ALU.mult, ALU.add)
        for a, b, o in two:
            tr(v("gs", 4 * a, 4 * b), v("so", 4 * a + o + 12, 4 * b + o + 12))
        publish(0, s, "YS")
        for a, b, o in two:
            copy("V", v("lf", a // 2 + 1, b // 2, 2) if r == 0 else v("la", a // 4, b // 4), v("so", 4 * a + o + 12, 4 * b + o, 16))
        for b in range(4):
            mm(4 + b, "eq", "ep", 128 * b, "lq" + s, "lp" + s, 0, C)
        for b in range(4):
            copy("SVVV"[b], tabv(b, 3 * C, 4 * C), v("ps", 512 * (4 + b), 512 * (4 + b) + C))
        late = [late_loads] if t == 0 else []
        lays = [lay(s, ds) for ds in ((1,), (-1,), (2, 3), (-2, -3))]
        after = ({0: lays + late}, {0: lays[:2], 2: lays[2:] + late}, {0: lays[:1], 2: lays[1:2], 4: lays[2:3], 6: lays[3:] + late},
                 {0: lays[:1], 2: lays[1:2], 4: lays[2:3], 6: lays[3:], 10: late})[r]
        for f in after[0]:
            f()
        for st in range(1, 4 * r + 1):
            w = max(0, (st - 3) // 2) % 2
            j = st // 2
            pub = st % 2 == 0 and j < 2 * r
            src = HC * j if pub else 0
            for h in range(3):
                copy("S", v("gs", src + 64 * h, src + 64 * h + 64), v("ww", M * w, M * w + M), v("la", 4 * h, 4 * h + 4))
            if pub:
                publish(j, s, "Y")
            for h in range(4):
                if h < 3:
                    tr(v("ts", 64 * h, 64 * h + 64), v("gs", src + 64 * h, src + 64 * h + 64))
                if h > 0 and st == 4 * r:
                    ts(v("lf", 8 * h - 7, 8 * h, 2), v("ts", 64 * h - 64, 64 * h, 16), float(M), ALU.add)
                elif h > 0:
                    copy("V", v("la", 4 * h - 4, 4 * h), v("ts", 64 * h - 64, 64 * h, 16))
            if st == 4 * r - 2:
                copy("V", v("lf", 0, 24, 2), v("ts", 0, HC, 16))
            for f in after.get(st, []):
                f()
        for h in range(3):
            copy("SVS"[h], v("gf", 128 * h, 128 * h + 128), v("ww", 0, 2 * M), v("lf", 8 * h, 8 * h + 8))
        for h in range(3):
            tr(v("tf", 128 * h, 128 * h + 128), v("gf", 128 * h, 128 * h + 128))
        for i, k in enumerate(order):
            for e in range(2):
                c0 = HC * (k % 2) + 32 * (k // 2) + 16 * e
                ts(v("ld", 6 * i + e, 6 * i + 6, 2), v("tf", c0, c0 + 129, 64), SLOT, ALU.add)

        def pick(a, b, engs="VVSS", xs=(2, 0, 3, 1)):
            for x in xs:
                copy(engs[x], v("ug" + s, 64 * a + x, 64 * b, 4), tabv(x, 0, TW), v("ld", a, b))

        def part(blocks, x):
            f = u8 if x == "q" else (lambda y: y)
            send([(order[i], es) for i, es in blocks], [f(v("ggb"[i] + x + s, 96 * i, 96 * i + 96)) for i, es in blocks],
                 [f(v("m" + x + s, 224, 320)) for i, es in blocks], "p2arr%d_%d" % (t, r))
        if not last:
            pick(0, 24)
            quant("gq" + s, "gp" + s, "ug" + s, C)
            send_tiles("g%s" + s, "m%s" + s, lambda k: p2place(r, k), "p2arr%d_%d" % (t, r))
        else:
            es = topo.engines(core, cores[near])
            h2, h4 = len(es) // 2, len(es) // 4
            pick(0, 12)
            pick(12, 18, "VSSS", (2, 3, 1))
            quant("gq" + s, "gp" + s, "ug" + s, HC)
            pick(12, 18, "VSSS", (0,))
            part([(0, es[:h2]), (1, es[h2:])], "q")
            quant("bq" + s, "bp" + s, "ug" + s, 128, 160, 160)
            part([(0, es[:h4]), (1, es[h4:h2]), (2, es[h2:])], "p")
            part([(2, es)], "q")
            pick(18, 24)
        for k in others:
            c0 = p2place(k, r)
            n = n_tiles(k) if k < N - 1 else 3 * n_all(k) // (2 if r == near else 4)
            arrive("p2arr%d_%d" % (t, k), n, [v(x + s, c0, c0 + 96) for x in ("mq", "mp")])
        if t == 0:
            fill = [lambda: quant("vq", "vp", "vt", 128)]
        else:
            def pl_send():
                tt_(v("plsend", 0, 24), v("pw", 96, 120), v("pw", 56, 80), ALU.add)
                send(thirds(2), [v("plsend", 6 * order.index(k), 6 * order.index(k) + 6) for k in others],
                     [v("pland", 6 * r, 6 * r + 6) for k in others], "plarr")
                arrive("plarr", sum(n_each(k, 2) for k in others), [v("pland", 6 * k, 6 * k + 6) for k in others])
            fill = [lambda: ts(v("pw", 0, 24), v("ld", 0, 24), BACK, ALU.add),
                    lambda: (ts(v("pw", 32, 56), v("pw", 0, 24), 1.0 / 96, ALU.mult, 0.5 / 96 - 0.5, ALU.add),
                             ts(v("pw", 56, 80), v("pw", 0, 24), 1.0 / C, ALU.mult, 0.5 / C - 0.5, ALU.add)),
                    lambda: copy("V", v("pwi", 0, 48), v("pw", 32, 80)),
                    lambda: (ts(v("pw", 32, 56), v("pwi", 0, 24), 288.0, ALU.mult),
                             ts(v("pw", 56, 80), v("pwi", 24, 48), -1440.0, ALU.mult)),
                    lambda: tt_(v("pw", 96, 120), v("pw", 32, 56), v("pw", 0, 24), ALU.add),
                    pl_send]
        H, HQ, HP = "ht" + s, "hq" + s, "hp" + s
        XN, XQN, XSN = "xt%d" % (t + 1), "xq%d" % (t + 1), "xs%d" % (t + 1)
        for i, k in enumerate(others + [r] if last else [r] + others):
            if k != r:
                names, c0 = ("mq" + s, "mp" + s), p2place(k, r)
                lo = 96 if c0 == 128 else c0
            elif not last:
                names, c0, lo = ("gq" + s, "gp" + s), 96 * r, 96 * r
            else:
                names, c0, lo = ("oq" + s, "op" + s), 32, 0
            base = 4 * (i % 2)
            for b in (0, 2, 1, 3):
                mm(base + b, "eq", "ep", 128 * b, names[0], names[1], lo, 128)

            def unpack(engs, bs, qs):
                for b in bs:
                    for q in qs:
                        c = 512 * (base + b) + c0 - lo
                        copy(engs[b], v(H, 384 * q + b, 384 * q + 384, 4, 32 * k, 32 * k + 32), v("ps", c, c + 96, 1, 32 * q, 32 * q + 32))
            if last and i < 2:
                for b in (0, 2, 1, 3):
                    c = 512 * (base + b) + c0 - lo
                    copy("VVSS"[b], v("hs" + s, 384 * i + b, 384 * i + 384, 4), v("ps", c, c + 96))
                for q in range(4):
                    dma("Y", v(H, 384 * q, 384 * q + 384, 1, 32 * k, 32 * k + 32),
                        v("hs" + s, 384 * i, 384 * i + 384, 1, 32 * q, 32 * q + 32), "dh" + s)
                if i == 0:
                    quant("oq" + s, "op" + s, "ug" + s, 128, 256)
                else:
                    fill.pop(0)()
            elif i < N - 1:
                for h in range(2):
                    for b in (0, 2, 1, 3):
                        unpack(("VVSS", "VVSV")[h], (b,), (2 * h, 2 * h + 1))
                        if fill and (b == 3 or (last and b < 2)):
                            fill.pop(0)()
            else:
                unpack("VVSV", (0, 2, 1, 3), (0, 1))
                unpack("VVSS", (2, 0, 1), (2,))
                unpack("VVSS", (2,), (3,))
                quant(HQ, HP, H, 128)
                unpack("VVSS", (3,), (2, 3))
                unpack("VVSS", (0, 1), (3,))
                quant(HQ, HP, H, 128, 128, 128)
                quant(HQ, HP, H, 128, 256, 256)

        def layer(h):
            for b in (2, 0, 3, 1):
                mm(4 * (h % 2) + b, "wq", "wp", 128 * b, HQ, HP, 128 * h, 128)
        layer(0)
        layer(1)
        for h in range(3):
            for b in (2, 0, 3, 1):
                o, a = v(XN, 512 * h + b, 512 * (h + 1), 4), v("ps", 512 * (4 * (h % 2) + b), 512 * (4 * (h % 2) + b) + 128)
                if b < 2:
                    ts(o, a, 0.0, ALU.max, 0.03125, ALU.mult)
                else:
                    add("S", lambda q, o=o, a=a: q.activation(o[0], a[0], AF.Relu, scale=0.03125), [o], [a])
            if h == 0:
                layer(2)
            if t == ROUNDS - 1 and h == 2:
                copy("V", v("in2", 6 * r, 6 * r + 6), v("plsend", 6 * r, 6 * r + 6))
                for a, b in ((0, 6 * r), (6 * r + 6, 24)):
                    if a < b:
                        copy("V", v("in2", a, b), v("pland", a, b))
            quant(XQN, XSN, XN, 128, 128 * h, 128 * h)
            if t < ROUNDS - 1 and h == 1:
                for x in range(2):
                    mm(4 + x, XQN, XSN, 128 * x, "uq", "up", 0, 128)
                for k in range(4):
                    for q in range(2):
                        dma("Y", v("sh1", 384 * k, 384 * k + 384, 1, 32 * q, 32 * q + 32),
                            v(XN, 384 * q, 384 * q + 384, 1, 32 * k, 32 * k + 32), "dsh1")
            if t == ROUNDS - 1 and h == 1:
                mm(4, "vq", "vp", 0, "xq2", "xs2", 0, 256)
                dma("Y", hbm(T.oc[:, 0:1024]), u8(v("xq2", 0, 256)), "doc")

    mm(5, "vq", "vp", 0, "xq2", "xs2", 256, 128)
    tr(v("plt", 0, 32), v("in2", 0, 32))
    copy("S", v("ysb", 0, 256), v("ps", 2048, 2048 + 256))
    copy("V", v("ysb", 256, C), v("ps", 2560, 2560 + 128))
    dma("S", hbm(T.y[:, 0:256]), v("ysb", 0, 256), "dy")
    dma("Y", hbm(T.oc[:, 1024:4 * C]), u8(v("xq2", 256, C)), "doc")
    for k in range(4):
        dma("YS"[k % 2], hbm(T.osc[4 * k:4 * k + 4, :]), v("xs2", 0, C, 1, 32 * k, 32 * k + 4), "doc")
    for q in range(4):
        for e in range(2):
            if (q, e) == (3, 1):
                dma("Y", hbm(T.y[:, 256:C]), v("ysb", 256, C), "dy")
            dma("SY"[e], hbm(T.pl[e:8:2, 96 * q:96 * q + 96]), v("plt", 16 * e, 16 * e + 16, 1, 32 * q, 32 * q + 24), "dpl")

    def meet(a, b):
        return a[0] == b[0] and a[1] < b[2] and b[1] < a[2] and not a[3].isdisjoint(b[3])

    seen, need, count, waited = {}, set(), {}, {}
    for i, op in enumerate(ops):
        deps = set(op["a"])
        for regs, mine in ((op["w"], True), (op["r"], False)):
            for reg in regs:
                for j, other, wrote in seen.get(reg[0], []):
                    if ops[j]["e"] == "G" and ops[j]["sem"] is not None:
                        continue
                    clash = mine or wrote or (reg[0] == "ps" and ops[j]["e"] != op["e"])
                    if clash and j != i and meet(reg, other):
                        deps.add(j)
        op["d"] = set() if op["e"] == "X" else deps
        for regs, mine in ((op["w"], True), (op["r"], False)):
            for reg in regs:
                seen.setdefault(reg[0], []).append((i, reg, mine))
    for op in ops:
        latest = {}
        for j in op["d"]:
            if ops[j]["sem"] is None:
                latest[ops[j]["e"]] = max(latest.get(ops[j]["e"], -1), j)
        op["last"] = latest
        need.update(latest.values())
    for i, op in enumerate(ops):
        if op["sem"] is None and i in need:
            count[op["e"]] = count.get(op["e"], 0) + 1
            op["n"] = count[op["e"]]
    for i, op in enumerate(ops):
        if op["e"] == "X":
            continue
        q = queue[op["e"]]
        want = {"c" + e: ops[j]["n"] for e, j in op["last"].items()}
        want.update({ops[j]["sem"]: total[ops[j]["sem"]] for j in op["d"] if ops[j]["sem"] is not None})
        for name in sorted(want):
            if waited.get((op["e"], name), 0) < want[name]:
                q.wait_ge(T.sem[name], want[name])
                waited[(op["e"], name)] = want[name]
        ins = op["f"](q)
        if op["sem"] is None:
            if "n" in op:
                ins.then_inc(T.sem["c" + op["e"]], 1)
        elif op["sem"] != "sent":
            ins.then_inc(T.sem[op["sem"]], 16)
    for name in sorted(total):
        if max([n for (e, x), n in waited.items() if x == name] + [0]) < total[name]:
            g.wait_ge(T.sem[name], total[name])
